import numpy as np, ml_dtypes
CORES = [2,6,10,14,18,22,26,30]
N = 8
BF = ml_dtypes.bfloat16
def gentries(a):
    return np.ascontiguousarray(a.reshape(8, 16, -1).transpose(0, 2, 1)).reshape(8, -1)
def gtable(e):
    e = np.asarray(e); return np.ascontiguousarray(e.reshape(8, -1, 16).transpose(0, 2, 1)).reshape(128, -1).astype(np.int32)
M, B, H, ST = 256, 8, 3, 3
W = M * B
def parts(rng):
    c = np.minimum((W * np.exp2(-5 * rng.random((N, 8, 1, W))) * rng.random((N, 8, 16, W))).astype(np.int64), W - 1)
    a = np.exp2(5 * rng.random((N, 8, 16, 1))); q = rng.choice(np.array([1, 1, 1, 16, 256]), (N, 8, 16, 1))
    l = np.minimum((W * rng.random((N, 8, 16, W)) ** a).astype(np.int64), W - 1) & -q
    gap = np.minimum((W * (0.1 + 0.8 * rng.random((N, 8, 1, M))) * (0.5 + rng.random((N, 8, 16, M)))).astype(np.int64), W - 1)
    return c, l, gap, rng.integers(0, B, (N, 8, M))
def pack(c, l, gap, cur):
    return {"ck": np.ascontiguousarray(c.reshape(N, 128, W)).astype(np.int32), "la": np.ascontiguousarray(l.reshape(N, 128, W)).astype(np.int32),
            "gap": np.ascontiguousarray(gap.reshape(N, 128, M)).astype(np.int32), "cu": np.stack([gtable(a) for a in cur])}
def setup_inputs(rng):
    return pack(*parts(rng))
def setup_inputs_ties(rng):
    c, l, gap, cur = parts(rng); c = c & -64; gap = gap & -64; l = l & -64
    kind = rng.integers(0, 4, (N, 8, 16, 1)); kind[:, :, :4, 0] = np.arange(4)
    few = np.take_along_axis(rng.integers(0, W, (N, 8, 16, 4)), rng.integers(0, kind + 1, (N, 8, 16, W)), 3)
    l[:, ::2] = few[:, ::2]
    gap = np.where((rng.random((N, 8, 1, M)) < 0.25) & (rng.random((N, 8, 16, M)) < 0.2), 0, gap)
    return pack(c, l, gap, cur)
def setup_inputs_alike(rng):
    c, l, gap, cur = parts(rng)
    c[:, ::2] = np.maximum(c[:, ::2, :1], 16); c[:, ::2, :, 0] = rng.integers(0, 16, (N, 4, 16))
    c[:, 1::2] = rng.choice(np.array([3, W // 3, W // 2, W - 1]), (N, 4, 16, W))
    cur[:, :, 0] = 0; gap[:, :, :, 0] = 0
    return pack(c, l, gap, cur)
def setup_inputs_ends(rng):
    c, l, gap, cur = parts(rng)
    c[:, 0:4] = rng.choice(np.array([0, 1, W - 2, W - 1]), (N, 4, 16, W))
    l[:, 2:6] = rng.choice(np.array([0, 1, W - 2, W - 1]), (N, 4, 16, W))
    gap[:, 1:7] = rng.choice(np.array([0, 1, W - 1]), (N, 6, 16, M))
    cur = rng.choice(np.array([0, B - 1]), (N, 8, M))
    return pack(c, l, gap, cur)
def setup_inputs_count(rng):
    c, l, gap, cur = parts(rng); c = np.maximum(c, 1)
    n = rng.choice(np.array([0, H - 1, H, H + 1, 16]), (N, 8, 1, M)); g = rng.permutation(8)
    n[:, g[0]] = 16; n[:, g[1]] = 0; n[:, g[2], 0, :5] = np.array([0, H - 1, H, H + 1, 16])
    cur[:, g[0], :B] = np.arange(B)
    n[0::2, g[3]] = 16; n[1::2, g[3]] = 0
    n[:, g[4]] = 16; l[:, g[4]] = l[:, g[4], :, :1].copy(); c[:, g[4], :, 0] = 0
    cur[:, g[4], 0] = 1; cur[:, g[4], 1:9] = (2 * np.arange(N)[:, None] + np.arange(8)) & (B - 1)
    gap = np.where(np.argsort(rng.random((N, 8, 16, M)), axis=2) < n, 0, W - 1)
    return pack(c, l, gap, cur)
def setup_inputs_spread(rng):
    c, l, gap, cur = parts(rng); e = np.log2(W)
    c = np.minimum((np.exp2(e * rng.random((N, 8, 1, W))) * rng.random((N, 8, 16, W))).astype(np.int64), W - 1)
    l = np.minimum(np.exp2(e * rng.random((N, 8, 16, W)) ** (2 * rng.random((N, 8, 16, 1)))).astype(np.int64), W - 1)
    gap = np.minimum((np.exp2(e * (1 - rng.random((N, 8, 1, M)) ** 3)) * rng.random((N, 8, 16, M))).astype(np.int64), W - 1)
    return pack(c, l, gap, cur)
def check_inputs(d):
    bad = []
    for k, hi in (("ck", W - 1), ("la", W - 1), ("gap", W - 1), ("cu", B - 1)):
        if np.min(d[k]) < 0 or np.max(d[k]) > hi: bad.append("range of " + k)
    return bad
def columns(t, x):
    return np.take_along_axis(t, np.swapaxes(x, 2, 3).reshape(N, 8, 1, 16 * M), 3).reshape(N, 8, 16, M, 16)
def reference(ck, la, gap, cu):
    C = ck.astype(np.int64).reshape(N, 8, 16, W); L = la.astype(np.int64).reshape(N, 8, 16, W); G = gap.astype(np.int64).reshape(N, 8, 16, M)
    cur = np.stack([gentries(a) for a in cu]).astype(np.int64); first = B * np.arange(M)
    I = np.take_along_axis(C, (first + cur)[:, :, None, :], 3); T = I + G
    for step in range(ST):
        A = columns(L, I); top = np.max(A, axis=4, keepdims=True)
        s = np.max(np.where(A < top, A, 0), axis=4)
        I = np.maximum(I, np.max(columns(C, s), axis=4))
        out = np.add.reduce((I >= T).astype(np.int64), axis=2) >= H
        hit = (np.arange(B) == cur[..., None]) & out[..., None]
        C = np.where(hit[:, :, None], I[..., None], C.reshape(N, 8, 16, M, B)).reshape(N, 8, 16, W)
        cur = np.where(out, (cur + 1) & (B - 1), cur)
        new = np.take_along_axis(C, (first + cur)[:, :, None, :], 3)
        T = np.where(out[:, :, None], new + G, T); I = np.where(out[:, :, None], new, I)
        I, T, G, cur = np.roll(I, 1, axis=0), np.roll(T, 1, axis=0), np.roll(G, 1, axis=0), np.roll(cur, 1, axis=0)
    return {"yi": I.reshape(N, 128, M).astype(np.float32), "yc": np.stack([gtable(a) for a in cur]).astype(np.float32)}

@@ -1,0 +1,377 @@
+from concourse.mybir import dt, AluOpType, ActivationFunctionType
+
+NQ, CH, ST, W = 4, 64, 3, 2048
+CW = CH * 16
+NC = NQ * CH
+HV, TV = 32, 16
+KB = 4608.0
+BIG = 4096.0
+SCHED = """
+L001 P0 R0 L011 l00 M00 U000 l01 M01 W000 U001 W001 L02 M02 S00 U010 W010 k00 U011 W011 L03 M03 S01 U020 W020 k01 U021 W021 C00
+m00 U030 S02 C01 U031 G00 k02 g00 B00 W030 E00 W031 H00 m01 J00 S03 k03 C02 F00 G01 g01 m02 B01 E01 G02 H01 J01 g02 F01 C03 m03
+B02 E02 G03 H02 g03 F02 J02 p0 v0 B03 E03 F03 d0 H03 L10 K00 J03 s0 M10 U100 U101 z0 K01 y0 K03 K02 L11 x0 M11 W100 L12 W101
+U111 M12 S10 L13 W111 k10 U110 W110 M13 S11 U120 W120 k11 U121 W121 C10 m10 U130 W130 P1 G10 S12 g10 k12 C11 U131 W131 R1 B10
+E10 F10 H10 J10 C12 m11 S13 G11 k13 C13 g11 B11 E11 F11 H11 K11 J11 m12 G12 g12 m13 B12 E12 G13 H12 g13 L20 F12 B13 L21 p1 J12
+L22 M20 U200 E13 F13 K12 H13 K13 J13 v1 K10 W200 d1 s1 L23 U201 M21 U211 z1 U210 W201 y1 S20 x1 k20 C20 M22 W211 W210 M23 R2
+S21 U220 W220 k21 C21 U221 W221 m20 S22 U230 W230 U231 k22 W231 P2 G20 S23 C22 g20 B20 m21 k23 G21 E20 g21 m22 c23 G22 C23 B21
+E21 m23 g22 G23 g23 e2 B22 E22 p2 H20 v2 B23 E23 H22 H21 H23 d2 s2 z2
+"""
+
+SCRATCH = {
+    "Lt": ("sbuf", [128, W], "int32"),
+    "Cx": ("sbuf", [128, W + NC], "int32"),
+    "gapi": ("sbuf", [128, NC], "int32"),
+    "cui": ("sbuf", [128, 16], "int32"),
+    "ones": ("sbuf", [128, 128], "float32"),
+    "tI": ("sbuf", [128, 128], "float32"),
+    "tB": ("sbuf", [128, 128], "float32"),
+    "tC": ("sbuf", [128, 128], "float32"),
+    "tD": ("sbuf", [128, 128], "float32"),
+    "tF": ("sbuf", [128, 128], "float32"),
+    "mask": ("sbuf", [128, CW], "float16"),
+    "IDh": ("sbuf", [128, 128], "float16"),
+    "NKh": ("sbuf", [128, 128], "float16"),
+    "PKh": ("sbuf", [128, 128], "float16"),
+    "BGh": ("sbuf", [128, 128], "float16"),
+    "NBh": ("sbuf", [128, 128], "float16"),
+    "Bh": ("sbuf", [128, 128], "float16"),
+    "Ah": ("sbuf", [128, 2 * 128], "float16"),
+    "TH": ("sbuf", [128, 2 * 128], "float32"),
+    "tj": ("sbuf", [128, 2 * 128], "int32"),
+    "tk": ("sbuf", [128, 2 * 128], "int32"),
+    "te": ("sbuf", [128, 2 * 128], "float32"),
+    "CSh": ("sbuf", [128, 64], "float16"),
+    "j8": ("sbuf", [128, 16], "int32"),
+    "jq": ("sbuf", [128, 16], "int32"),
+    "j8a": ("sbuf", [128, 16], "int32"),
+    "i8": ("sbuf", [128, 16], "int32"),
+    "ic": ("sbuf", [128, 16], "int32"),
+    "cr": ("sbuf", [128, 64], "int32"),
+    "cm": ("sbuf", [128, 64], "int32"),
+    "ou": ("sbuf", [128, 32], "uint16"),
+    "I0": ("sbuf", [128, NC], "float16"),
+    "SL": ("sbuf", [128, NC], "uint16"),
+    "NEW": ("sbuf", [128, NC], "float16"),
+    "GE": ("sbuf", [128, NC], "float16"),
+    "REL": ("sbuf", [128, NC], "float16"),
+    "A2": ("sbuf", [128, NC], "float16"),
+    "A3": ("sbuf", [128, NC], "float16"),
+    "lt2": ("sbuf", [128, 64], "float32"),
+    "EC": ("sbuf", [128, 32], "float32"),
+    "YO": ("sbuf", [128, NC], "float32"),
+    "YL": ("sbuf", [128, NC], "float32"),
+    "YCL": ("sbuf", [128, 16], "float32"),
+    "U0": ("psum", [128, 1024], "float32"),
+    "U1": ("psum", [128, 1024], "float32"),
+    "BK": ("psum", [128, 512], "float32"),
+    "TB": ("psum", [128, 512], "float32"),
+    "AB": ("psum", [128, 512], "float32"),
+}
+for _q in range(NQ):
+    for _n in ("X", "R", "Wm", "S2", "Y", "R2"):
+        SCRATCH["%s%d" % (_n, _q)] = ("sbuf", [128, CW], "float16")
+for _t in range(ST):
+    SCRATCH["LI%d" % _t] = ("sbuf", [128, NC], "uint16")
+    SCRATCH["GP%d" % _t] = ("sbuf", [128, NC], "float16")
+    SCRATCH["E%d" % _t] = ("sbuf", [128, 80], "float32")
+    SCRATCH["RES%d" % _t] = ("sbuf", [128, 64], "float32")
+    if _t:
+        SCRATCH["IB%d" % _t] = ("sbuf", [128, 2 * NC], "float16")
+        SCRATCH["NU%d" % _t] = ("sbuf", [128, 16], "uint16")
+    if _t < ST - 1:
+        SCRATCH["OL%d" % _t] = ("sbuf", [128, NC], "uint16")
+        SCRATCH["OB%d" % _t] = ("sbuf", [128, 2 * NC], "float16")
+        SCRATCH["RU%d" % _t] = ("sbuf", [128, 48], "uint16")
+
+SEMAPHORES = ["sv", "ss", "sp", "sg", "dck", "dla", "dcu", "dgp", "loc", "ag1", "ag2", "dout", "dyc", "ayc"]
+for _t in (1, 2):
+    SEMAPHORES += ["ae%d" % _t, "an%d" % _t]
+    for _q in range(NQ):
+        SEMAPHORES += ["al%d_%d" % (_t, _q), "ab%d_%d" % (_t, _q)]
+SEMAPHORES += ["ay%d" % _q for _q in range(NQ)]
+
+
+def rank_program(g, core, T, topo):
+    rank = T.rank_of(core)
+    if rank is None:
+        return
+    A, COPY = AluOpType, ActivationFunctionType.Copy
+    cores = list(T.cores)
+    n = len(cores)
+    nxt, nx2, prv, pv2 = cores[(rank + 1) % n], cores[(rank + 2) % n], cores[(rank - 1) % n], cores[(rank - 2) % n]
+    V, S, P = g.vector, g.scalar, g.tensor
+    que = {"v": V, "s": S, "p": P, "g": g, "y": g.sync}
+    own = {"v": "sv", "s": "ss", "p": "sp", "g": "sg"}
+    cnt = {"v": 0, "s": 0, "p": 0, "g": 0}
+    known, wr, rd, tot = {}, {}, {}, {"loc": 0}
+
+    def wait(q, sem, val):
+        if known.get((q, sem), 0) < val:
+            que[q].wait_ge(T.sem[sem], val)
+            known[(q, sem)] = val
+
+    def deps(q, r, w):
+        need = {}
+        mine = own.get(q)
+        for k in r:
+            if k in wr:
+                sem, val = wr[k]
+                if not (q == "p" and sem == mine):
+                    need[sem] = max(need.get(sem, 0), val)
+        for k in w:
+            toks = dict(rd.get(k, {}))
+            toks.pop(mine, None)
+            if k in wr and not (q == "p" and wr[k][0] == mine):
+                toks[wr[k][0]] = max(toks.get(wr[k][0], 0), wr[k][1])
+            for sem, val in toks.items():
+                need[sem] = max(need.get(sem, 0), val)
+        for sem, val in need.items():
+            wait(q, sem, val)
+
+    def op(q, fn, r=(), w=()):
+        deps(q, r, w)
+        fn().then_inc(T.sem[own[q]], 1)
+        cnt[q] += 1
+        for k in r:
+            rd.setdefault(k, {})[own[q]] = cnt[q]
+        for k in w:
+            wr[k] = (own[q], cnt[q])
+            rd[k] = {}
+
+    def load(q, out, in_, sem, key):
+        que[q].dma_start(out, in_).then_inc(T.sem[sem], 16)
+        wr[key] = (sem, 16)
+
+    def send(dst, out, in_, sem, r):
+        deps("g", r, ())
+        rid, pid, _ = topo.addr(dst)
+        g.remote_dma(out, in_, T.sem[sem], T.sem.loc, pid, rid, topo.mask(core, dst))
+        tot["loc"] += len(topo.engines(core, dst))
+
+    def lands(src, sem, key):
+        wr[key] = (sem, len(topo.engines(src, core)))
+
+    def arr(name, k):
+        return T["%s%d" % (name, k)]
+
+    load("s", T.cui[:], T.cu[:], "dcu", "cui")
+    load("y", T.Cx[:, 0:W], T.ck[:], "dck", "C")
+    load("s", T.gapi[:], T.gap[:], "dgp", "gapi")
+    load("y", T.Lt[:], T.la[:], "dla", "Lt")
+    for t in (1, 2):
+        lands(prv, "ae%d" % t, ("E", t))
+        lands(prv, "an%d" % t, ("NU", t))
+        for q in range(NQ):
+            lands(prv, "al%d_%d" % (t, q), ("LI", t, q))
+            lands(prv, "ab%d_%d" % (t, q), ("IB", t, q))
+    lands(prv, "ag1", ("GP", 1))
+    lands(pv2, "ag2", ("GP", 2))
+
+    op("g", lambda: g.iota(T.j8[:], [[0, 16]], 0, 8), w=["j8"])
+    op("g", lambda: g.iota(T.jq[:], [[128, 16]], 0, 0), w=["jq"])
+    op("v", lambda: V.memset(T.ones[:], 1.0), w=["ones"])
+    op("g", lambda: g.affine_select(T.tI[:], T.ones[:], [[-1, 128]], A.is_equal, 0.0, 0, 1), r=["ones"], w=["tI"])
+    op("g", lambda: g.affine_select(T.tC[:], T.ones[:], [[-16, 8], [0, 16]], A.is_ge, 0.0, 0, 1), r=["ones"], w=["tC"])
+    op("g", lambda: g.affine_select(T.tB[:], T.tC[:], [[16, 8], [0, 16]], A.is_ge, 0.0, 15, -1), r=["tC"], w=["tB"])
+    op("g", lambda: g.iota(T.tj[:], [[0, 2], [-1, 128]], 128, 1), w=["tj"])
+    for h in range(2):
+        hs = slice(64 * h, 64 * h + 64)
+        op("g", lambda: g.affine_select(T.tD[:, hs], T.ones[:, hs], [[0, 4], [-16, 16]], A.is_ge, 0.0, 128 * h, 1), r=["ones"], w=[("tD", h)])
+        op("g", lambda: g.affine_select(T.tF[:, hs], T.tD[:, hs], [[0, 4], [16, 16]], A.is_ge, 0.0, 15 - 128 * h, -1), r=[("tD", h)], w=[("tF", h)])
+    op("v", lambda: V.memset(T.mask[:], 1.0), w=["mask"])
+    op("v", lambda: V.memset(T.mask[:, 0::16], 0.0), w=["mask"])
+    op("v", lambda: V.memset(T.CSh[:], -2.5 / 16), w=["CSh"])
+    op("v", lambda: V.tensor_scalar(T.j8a[:], T.j8[:], 127, None, A.bitwise_and), r=["j8"], w=["j8a"])
+    op("v", lambda: V.tensor_tensor(T.i8[:], T.j8a[:], T.jq[:], A.add), r=["j8a", "jq"], w=["i8"])
+    op("v", lambda: V.tensor_scalar(T.ic[:], T.i8[:], 3, None, A.logical_shift_right), r=["i8"], w=["ic"])
+    op("v", lambda: V.tensor_scalar(T.E0[:, 0:16], T.ic[:], W, None, A.add), r=["ic"], w=[("E0", 4)])
+    op("v", lambda: V.tensor_scalar(T.E1[:, 0:16], T.ic[:], W, None, A.add), r=["ic"], w=["E1d"])
+    op("v", lambda: V.tensor_copy(T.IDh[:], T.tI[:]), r=["tI"], w=["IDh"])
+    op("v", lambda: V.tensor_scalar(T.NKh[:], T.tI[:], -float(W), None, A.mult), r=["tI"], w=["NKh"])
+    op("v", lambda: V.tensor_scalar(T.PKh[:], T.tI[:], float(W), None, A.mult), r=["tI"], w=["PKh"])
+    op("v", lambda: V.tensor_scalar(T.BGh[:], T.tB[:], KB, None, A.mult), r=["tB"], w=["BGh"])
+    op("v", lambda: V.tensor_scalar(T.NBh[:], T.tB[:], -KB, None, A.mult), r=["tB"], w=["NBh"])
+    for k in range(4):
+        op("v", lambda: V.tensor_scalar(T.cr[:, 16 * k:16 * k + 16], T.cui[:], k, None, A.add), r=["cui"], w=[("cr", k)])
+    op("v", lambda: V.tensor_scalar(T.cm[:], T.cr[:], 7, None, A.bitwise_and), r=[("cr", k) for k in range(4)], w=["cm"])
+    for k in range(4):
+        op("v", lambda: V.tensor_tensor(T.E0[:, 16 + 16 * k:32 + 16 * k], T.cm[:, 16 * k:16 * k + 16], T.i8[:], A.add),
+           r=["cm", "i8"], w=[("E0", k)])
+    op("v", lambda: V.tensor_copy(T.ou[:], T.E0[:, 16:48]), r=[("E0", 0), ("E0", 1)], w=["ou"])
+    op("v", lambda: V.tensor_copy(T.LI0[:], T.Cx[:, 0:W].indirect(T.ou[:, 0:16])), r=["C", "ou"],
+       w=[("LI", 0, q) for q in range(NQ)])
+    op("v", lambda: V.tensor_copy(T.I0[:], T.LI0[:]), r=[("LI", 0, q) for q in range(NQ)], w=[("IB", 0, q) for q in range(NQ)])
+    op("v", lambda: V.tensor_copy(T.GP0[:], T.gapi[:]), r=["gapi"], w=[("GP", 0)])
+    send(nxt, T.GP1[:], T.GP0[:], "ag1", [("GP", 0)])
+    send(nx2, T.GP2[:], T.GP0[:], "ag2", [("GP", 0)])
+    op("v", lambda: V.tensor_scalar(T.tk[:], T.tj[:], 15, None, A.bitwise_and), r=["tj"], w=["tk"])
+    op("v", lambda: V.tensor_scalar(T.te[:], T.tk[:], 0, None, A.is_equal), r=["tk"], w=["te"])
+    op("v", lambda: V.tensor_scalar(T.TH[:], T.te[:], -1048576.0, 1048576.0 + 2.5 * KB, A.mult, A.add), r=["te"], w=["TH"])
+    op("v", lambda: V.tensor_scalar(T.Bh[:], T.tF[:], BIG, None, A.mult), r=[("tF", 0), ("tF", 1)], w=["Bh"])
+
+    def cols(q):
+        return slice(CH * q, CH * q + CH)
+
+    def iap(t, q):
+        return T.I0[:, cols(q)] if t == 0 else arr("IB", t)[:, 2 * CH * q:2 * CH * q + CH]
+
+    def bap(t, q):
+        return T.I0[:, cols(q)] if t == 0 else arr("IB", t)[:, 2 * CH * q + CH:2 * CH * q + 2 * CH]
+
+    def a1(q):
+        return T.AB[:, 256 + CH * q:256 + CH * q + CH]
+
+    def Lg(t, q, b=0):
+        k = HV * b
+        op("s", lambda: S.activation(arr("X", q)[:, 16 * k:CW], T.Lt[:, 0:W].indirect(arr("LI", t)[:, CH * q + k:CH * q + CH]), COPY),
+           r=["Lt", ("LI", t, q)], w=[("X", q, 1)] if b else [("X", q, 0), ("X", q, 1)])
+
+    def Lv(t, q):
+        op("v", lambda: V.tensor_copy(arr("X", q)[:, 0:16 * HV], T.Lt[:, 0:W].indirect(arr("LI", t)[:, CH * q:CH * q + HV])),
+           r=["Lt", ("LI", t, q)], w=[("X", q, 0)])
+
+    def Mx(t, q):
+        op("v", lambda: V.tensor_tensor_scan(arr("R", q)[:], T.mask[:], arr("X", q)[:], 0.0, A.mult, A.max),
+           r=["mask", ("X", q, 0), ("X", q, 1)], w=[("R", q)])
+
+    def Ug(t, q, b):
+        for k in range(8 * b, 8 * b + 8):
+            o, key = arr("U", q % 2)[:, CH * k:CH * k + CH], ("U", q % 2, b)
+            op("p", lambda: P.matmul(o, T.NKh[:], arr("X", q)[:, k::16], True, False), r=["NKh", ("X", q, 0), ("X", q, 1)], w=[key])
+            op("p", lambda: P.matmul(o, T.PKh[:], arr("R", q)[:, 15::16], False, True), r=["PKh", ("R", q)], w=[key])
+
+    def Wm(t, q, b):
+        for k in range(8 * b, 8 * b + 8):
+            op("v", lambda: V.tensor_tensor(arr("Wm", q)[:, k::16], arr("X", q)[:, k::16], arr("U", q % 2)[:, CH * k:CH * k + CH], A.min),
+               r=[("X", q, 0), ("X", q, 1), ("U", q % 2, b)], w=[("Wm", q, k)])
+
+    def Sc(t, q):
+        op("v", lambda: V.tensor_tensor_scan(arr("S2", q)[:], T.mask[:], arr("Wm", q)[:], 0.0, A.mult, A.max),
+           r=["mask"] + [("Wm", q, k) for k in range(16)], w=[("S2", q)])
+
+    def Sk(t, q):
+        op("v", lambda: V.tensor_copy(T.SL[:, cols(q)], arr("S2", q)[:, 15::16]), r=[("S2", q)], w=[("SL", q)])
+
+    def Cg(t, q):
+        k = TV if (t, q) == (ST - 1, NQ - 1) else 0
+        op("s", lambda: S.activation(arr("Y", q)[:, 16 * k:CW], T.Cx[:, 0:W].indirect(T.SL[:, CH * q + k:CH * q + CH]), COPY),
+           r=["C", ("SL", q)], w=[("Y", q)])
+
+    def Cv(t, q):
+        op("v", lambda: V.tensor_copy(arr("Y", q)[:, 0:16 * TV], T.Cx[:, 0:W].indirect(T.SL[:, CH * q:CH * q + TV])),
+           r=["C", ("SL", q)], w=[("Yv", q)])
+
+    def Rl(t):
+        if t == 0:
+            op("v", lambda: V.tensor_copy(T.REL[:], T.Cx[:, 0:W].indirect(T.ou[:, 16:32])), r=["C", "ou"], w=["REL"])
+        else:
+            op("s", lambda: S.activation(T.REL[:], T.Cx[:, 0:W].indirect(arr("NU", t)[:]), COPY), r=["C", ("NU", t)], w=["REL"])
+
+    def PTI(t):
+        for q in range(NQ):
+            op("p", lambda: P.matmul(T.AB[:, cols(q)], T.IDh[:], iap(t, q), True, True), r=["IDh", ("IB", t, q)], w=["AB"])
+        for q in range(NQ):
+            op("p", lambda: P.matmul(T.TB[:, cols(q)], T.IDh[:], bap(t, q), True, False), r=["IDh", ("IB", t, q)], w=["TB"])
+            op("p", lambda: P.matmul(T.TB[:, cols(q)], T.IDh[:], arr("GP", t)[:, cols(q)], False, True), r=[("GP", t)], w=["TB"])
+
+    def Cm(t, q):
+        op("v", lambda: V.tensor_tensor_scan(arr("R2", q)[:], T.mask[:], arr("Y", q)[:], 0.0, A.mult, A.max),
+           r=["mask", ("Y", q), ("Yv", q)], w=[("R2", q)])
+
+    def Ge(t, q):
+        op("v", lambda: V.tensor_tensor(T.NEW[:, cols(q)], arr("R2", q)[:, 15::16], T.AB[:, cols(q)], A.max),
+           r=[("R2", q), "AB"], w=[("NEW", q)])
+
+    def Gb(t, q):
+        op("v", lambda: V.tensor_tensor(T.GE[:, cols(q)], T.NEW[:, cols(q)], T.TB[:, cols(q)], A.is_ge),
+           r=[("NEW", q), "TB"], w=[("GE", q)])
+
+    def Pb(t, q):
+        for k, m in ((0, "BGh"), (1, "NBh")):
+            op("p", lambda: P.matmul(T.BK[:, CH * k:CH * k + CH], T[m][:], T.CSh[:, 0:CH], True, False), r=[m, "CSh"], w=["BK"])
+            op("p", lambda: P.matmul(T.BK[:, CH * k:CH * k + CH], T[m][:], T.GE[:, cols(q)], False, True), r=[m, ("GE", q)], w=["BK"])
+
+    def Se(t, q):
+        op("v", lambda: V.tensor_tensor(a1(q), T.REL[:, cols(q)], T.BK[:, 0:CH], A.min), r=["REL", "BK", "AB"], w=[("a1", q)])
+        op("v", lambda: V.tensor_tensor(T.A2[:, cols(q)], T.NEW[:, cols(q)], T.BK[:, CH:2 * CH], A.min), r=[("NEW", q), "BK"], w=[("A2", q)])
+
+    def Sh(t, q):
+        o = T.YO[:, cols(q)] if t == ST - 1 else arr("OB", t)[:, 2 * CH * q:2 * CH * q + CH]
+        op("v", lambda: V.tensor_tensor(o, T.A2[:, cols(q)], a1(q), A.max), r=[("A2", q), ("a1", q), "AB"], w=[("OBi", t, q)])
+        if t == ST - 1:
+            send(nxt, T.YL[:, cols(q)], T.YO[:, cols(q)], "ay%d" % q, [("OBi", t, q)])
+
+    def Sj(t, q):
+        op("v", lambda: V.tensor_copy(arr("OL", t)[:, cols(q)], arr("OB", t)[:, 2 * CH * q:2 * CH * q + CH]), r=[("OBi", t, q)], w=[("OL", t, q)])
+        send(nxt, arr("LI", t + 1)[:, cols(q)], arr("OL", t)[:, cols(q)], "al%d_%d" % (t + 1, q), [("OL", t, q)])
+
+    def Sf(t, q):
+        op("v", lambda: V.tensor_tensor(T.A3[:, cols(q)], bap(t, q), T.BK[:, CH:2 * CH], A.min), r=[("IB", t, q), "BK"], w=[("A3", q)])
+
+    def Sb(t, q):
+        ob = arr("OB", t)[:, 2 * CH * q + CH:2 * CH * q + 2 * CH]
+        op("v", lambda: V.tensor_tensor(ob, T.A3[:, cols(q)], a1(q), A.max), r=[("A3", q), ("a1", q), "AB"], w=[("OBb", t, q)])
+        send(nxt, arr("IB", t + 1)[:, 2 * CH * q:2 * CH * (q + 1)], arr("OB", t)[:, 2 * CH * q:2 * CH * (q + 1)], "ab%d_%d" % (t + 1, q),
+             [("OBi", t, q), ("OBb", t, q)])
+
+    def Pl(t):
+        for h in range(2):
+            op("p", lambda: P.matmul(T.TB[:, 256 + 128 * h:384 + 128 * h], T.GE[:, 128 * h:128 * h + 128], T.BGh[:], True, True),
+               r=["BGh"] + [("GE", q) for q in range(NQ)], w=["TB"])
+
+    def Vl(t):
+        op("v", lambda: V.tensor_tensor(T.Ah[:], T.TB[:, 256:512], T.TH[:], A.is_ge), r=["TB", "TH"], w=["Ah"])
+
+    def Pd(t):
+        w = 16 * (4, 3, 1)[t]
+        for h in range(2):
+            op("p", lambda: P.matmul(T.BK[:, 128:128 + w], T.Ah[:, 128 * h:128 * h + 128], T.Bh[:, 64 * h:64 * h + w], h == 0, h == 1),
+               r=["Ah", "Bh"], w=["BK"])
+
+    def Sl(t):
+        w = 16 * (4, 3, 1)[t]
+        e = T.EC if t == ST - 1 else arr("E", t)
+        src = [("E0", k) for k in range(5)] if t == 0 else [("E", t), "E1d"] if t == 1 else ["EC0", "EC1"]
+        op("v", lambda: V.tensor_tensor(T.BK[:, 192:192 + w], e[:, 16:16 + w], T.BK[:, 128:128 + w], A.min), r=src + ["BK"], w=["lt1"])
+        op("v", lambda: V.tensor_tensor(T.lt2[:, 0:w], e[:, 0:w], T.BK[:, 128:128 + w], A.subtract), r=src + ["BK"], w=["lt2"])
+
+    def Sz(t):
+        w = 16 * (4, 3, 1)[t]
+        res = arr("RES", t)
+        op("v", lambda: V.tensor_tensor(res[:, 0:w], T.lt2[:, 0:w], T.BK[:, 192:192 + w], A.max), r=["lt1", "lt2", "BK"], w=[("RES", t)])
+        if t == ST - 1:
+            send(nxt, T.YCL[:], res[:, 0:16], "ayc", [("RES", t)])
+
+    def Sy(t):
+        res = arr("RES", t)
+        op("v", lambda: V.tensor_copy(arr("RU", t)[:], res[:, 0:48]), r=[("RES", t)], w=[("RU", t)])
+        send(nxt, arr("NU", t + 1)[:], arr("RU", t)[:, 32:48], "an%d" % (t + 1), [("RU", t)])
+        if t == 0:
+            send(nxt, T.E1[:, 16:64], res[:, 16:64], "ae1", [("RES", t)])
+        else:
+            send(nxt, T.E2[:, 0:32], res[:, 16:48], "ae2", [("RES", t)])
+
+    def Scat(t):
+        op("v", lambda: V.tensor_copy(T.Cx[:, 0:W + NC].indirect(arr("RU", t)[:, 0:16]), T.NEW[:]),
+           r=[("RU", t)] + [("NEW", q) for q in range(NQ)], w=["C"])
+
+    def Ec(t):
+        for k in range(2):
+            op("v", lambda: V.tensor_tensor(T.EC[:, 16 * k:16 * k + 16], T.E2[:, 16 * k:16 * k + 16], T.i8[:], A.subtract),
+               r=[("E", 2), "i8"], w=["EC%d" % k])
+
+    parts = {"L": Lg, "l": Lv, "M": Mx, "U": Ug, "W": Wm, "S": Sc, "k": Sk, "C": Cg, "c": Cv, "R": Rl, "P": PTI, "m": Cm, "G": Ge, "g": Gb,
+             "B": Pb, "E": Se, "H": Sh, "J": Sj, "F": Sf, "K": Sb, "p": Pl, "v": Vl, "d": Pd, "s": Sl, "z": Sz, "y": Sy, "x": Scat, "e": Ec}
+    for tok in SCHED.split():
+        parts[tok[0]](*[int(c) for c in tok[1:]])
+
+    for q in range(NQ):
+        wait("y", "ay%d" % q, len(topo.engines(prv, core)))
+        g.sync.dma_start(T.yi[:, cols(q)], T.YL[:, cols(q)]).then_inc(T.sem.dout, 16)
+    wait("s", "ayc", len(topo.engines(prv, core)))
+    S.dma_start(T.yc[:], T.YCL[:]).then_inc(T.sem.dyc, 16)
+    wait("s", "dyc", 16)
+    wait("y", "dout", 16 * NQ)
+    for q in own:
+        wait("g", own[q], cnt[q])
+    wait("g", "loc", tot["loc"])

@@ -3,92 +3,90 @@ from concourse.mybir import dt, AluOpType, ActivationFunctionType
 NQ, CH, ST, W = 4, 64, 3, 2048
 CW = CH * 16
 NC = NQ * CH
-HV, TV = 32, 16
-KB = 4608.0
-BIG = 4096.0
-SCHED = """
-L001 P0 R0 L011 l00 M00 U000 l01 M01 W000 U001 W001 L02 M02 S00 U010 W010 k00 U011 W011 L03 M03 S01 U020 W020 k01 U021 W021 C00
-m00 U030 S02 C01 U031 G00 k02 g00 B00 W030 E00 W031 H00 m01 J00 S03 k03 C02 F00 G01 g01 m02 B01 E01 G02 H01 J01 g02 F01 C03 m03
-B02 E02 G03 H02 g03 F02 J02 p0 v0 B03 E03 F03 d0 H03 L10 K00 J03 s0 M10 U100 U101 z0 K01 y0 K03 K02 L11 x0 M11 W100 L12 W101
-U111 M12 S10 L13 W111 k10 U110 W110 M13 S11 U120 W120 k11 U121 W121 C10 m10 U130 W130 P1 G10 S12 g10 k12 C11 U131 W131 R1 B10
-E10 F10 H10 J10 C12 m11 S13 G11 k13 C13 g11 B11 E11 F11 H11 K11 J11 m12 G12 g12 m13 B12 E12 G13 H12 g13 L20 F12 B13 L21 p1 J12
-L22 M20 U200 E13 F13 K12 H13 K13 J13 v1 K10 W200 d1 s1 L23 U201 M21 U211 z1 U210 W201 y1 S20 x1 k20 C20 M22 W211 W210 M23 R2
-S21 U220 W220 k21 C21 U221 W221 m20 S22 U230 W230 U231 k22 W231 P2 G20 S23 C22 g20 B20 m21 k23 G21 E20 g21 m22 c23 G22 C23 B21
-E21 m23 g22 G23 g23 e2 B22 E22 p2 H20 v2 B23 E23 H22 H21 H23 d2 s2 z2
-"""
+NN = NQ * ST
+BANK = 512
+NUB = 2
+NQB = 7 - 2 * NUB
+OV = False
+HUGE = 2.0 ** 40
+ULP8 = 1.5 * 2.0 ** 26
+VL = {0: 32, 1: 16}
+VC = {3: 32, 7: 32, 11: 8}
+START = "I0 L0 l0 I1 M0 X0 U0 V0 L1 l1 A0 X1 i0 I2 L2 W0 Z0 M1 S0 I3 k0 U1 V1"
+STEP = ("C0 L3 R0 W1 Z1 M2 S1 m0 P1 P0 X2 U2 V2 i2 k1 G0 W2 C1 g0 Z2 B0 f0 Q0 S2 J0 M3 k2 C2 L4 P2 X3 U3 V3 m1 W3 G1 Z3 g1 m2 B1 o0 f1 G2 "
+        "S3 g2 Q1 B2 o1 P3 J1 k3 f2 Q2 O0 C3 L5 c3 M4 J2 X4 o2 V4 U4 m3 G3 g3 W4 B3 f3 Z4 Q3 u0 J3 S4 v0 M5 w0 X5 y0 k4 x0 i4 o3 U5 V5 L6 O2")
+LAST = ("W1 M2 P0 X2 U2 L3 i2 Z1 W2 V2 Z2 S1 C0 M3 X3 S2 k1 V3 P2 U3 P1 m0 Z3 G0 k2 R0 C1 W3 C2 g0 B0 S3 f0 Q0 m1 k3 G1 J0 g1 m2 B1 f1 Q1 "
+        "P3 G2 g2 c3 J1 B2 f2 C3 m3 Q2 G3 J2 g3 B3 f3 Q3 J3 u0 w0 y0")
 
 SCRATCH = {
     "Lt": ("sbuf", [128, W], "int32"),
-    "Cx": ("sbuf", [128, W + NC], "int32"),
+    "Cx": ("sbuf", [128, 2 * W], "int32"),
     "gapi": ("sbuf", [128, NC], "int32"),
     "cui": ("sbuf", [128, 16], "int32"),
     "ones": ("sbuf", [128, 128], "float32"),
     "tI": ("sbuf", [128, 128], "float32"),
     "tB": ("sbuf", [128, 128], "float32"),
     "tC": ("sbuf", [128, 128], "float32"),
-    "tD": ("sbuf", [128, 128], "float32"),
-    "tF": ("sbuf", [128, 128], "float32"),
     "mask": ("sbuf", [128, CW], "float16"),
     "IDh": ("sbuf", [128, 128], "float16"),
+    "NIh": ("sbuf", [128, 128], "float16"),
     "NKh": ("sbuf", [128, 128], "float16"),
     "PKh": ("sbuf", [128, 128], "float16"),
-    "BGh": ("sbuf", [128, 128], "float16"),
-    "NBh": ("sbuf", [128, 128], "float16"),
-    "Bh": ("sbuf", [128, 128], "float16"),
-    "Ah": ("sbuf", [128, 2 * 128], "float16"),
-    "TH": ("sbuf", [128, 2 * 128], "float32"),
-    "tj": ("sbuf", [128, 2 * 128], "int32"),
-    "tk": ("sbuf", [128, 2 * 128], "int32"),
-    "te": ("sbuf", [128, 2 * 128], "float32"),
-    "CSh": ("sbuf", [128, 64], "float16"),
+    "IDb": ("sbuf", [128, 128], "bfloat16"),
+    "BGb": ("sbuf", [128, 128], "bfloat16"),
+    "PHb": ("sbuf", [128, 128], "bfloat16"),
+    "NHb": ("sbuf", [128, 128], "bfloat16"),
+    "R8b": ("sbuf", [128, 256], "bfloat16"),
+    "oneb": ("sbuf", [128, 32], "bfloat16"),
+    "K1": ("sbuf", [128, 32], "float16"),
+    "K2": ("sbuf", [128, 32], "float16"),
+    "TH": ("sbuf", [128, CH], "float32"),
+    "tj": ("sbuf", [128, CH], "int32"),
+    "tk": ("sbuf", [128, CH], "int32"),
     "j8": ("sbuf", [128, 16], "int32"),
-    "jq": ("sbuf", [128, 16], "int32"),
+    "jq": ("sbuf", [128, 32], "int32"),
     "j8a": ("sbuf", [128, 16], "int32"),
-    "i8": ("sbuf", [128, 16], "int32"),
-    "ic": ("sbuf", [128, 16], "int32"),
-    "cr": ("sbuf", [128, 64], "int32"),
-    "cm": ("sbuf", [128, 64], "int32"),
+    "i8": ("sbuf", [128, 32], "int32"),
+    "ca": ("sbuf", [128, 16], "int32"),
+    "cb": ("sbuf", [128, 16], "int32"),
+    "cc": ("sbuf", [128, 32], "int32"),
     "ou": ("sbuf", [128, 32], "uint16"),
-    "I0": ("sbuf", [128, NC], "float16"),
     "SL": ("sbuf", [128, NC], "uint16"),
     "NEW": ("sbuf", [128, NC], "float16"),
-    "GE": ("sbuf", [128, NC], "float16"),
+    "GE": ("sbuf", [128, NC], "bfloat16"),
+    "FL": ("sbuf", [128, NC], "float16"),
     "REL": ("sbuf", [128, NC], "float16"),
-    "A2": ("sbuf", [128, NC], "float16"),
-    "A3": ("sbuf", [128, NC], "float16"),
-    "lt2": ("sbuf", [128, 64], "float32"),
-    "EC": ("sbuf", [128, 32], "float32"),
     "YO": ("sbuf", [128, NC], "float32"),
     "YL": ("sbuf", [128, NC], "float32"),
+    "YC": ("sbuf", [128, 16], "float32"),
     "YCL": ("sbuf", [128, 16], "float32"),
-    "U0": ("psum", [128, 1024], "float32"),
-    "U1": ("psum", [128, 1024], "float32"),
-    "BK": ("psum", [128, 512], "float32"),
-    "TB": ("psum", [128, 512], "float32"),
-    "AB": ("psum", [128, 512], "float32"),
+    "FD": ("sbuf", [128, NC], "bfloat16"),
+    "Z": ("psum", [128, BANK], "float32"),
 }
+for _q in range(NUB):
+    SCRATCH["U%d" % _q] = ("psum", [128, 2 * BANK], "float32")
+for _q in range(NQB):
+    SCRATCH["Q%d" % _q] = ("psum", [128, BANK], "float32")
 for _q in range(NQ):
     for _n in ("X", "R", "Wm", "S2", "Y", "R2"):
         SCRATCH["%s%d" % (_n, _q)] = ("sbuf", [128, CW], "float16")
 for _t in range(ST):
     SCRATCH["LI%d" % _t] = ("sbuf", [128, NC], "uint16")
+    SCRATCH["IH%d" % _t] = ("sbuf", [128, NC], "float16")
     SCRATCH["GP%d" % _t] = ("sbuf", [128, NC], "float16")
-    SCRATCH["E%d" % _t] = ("sbuf", [128, 80], "float32")
-    SCRATCH["RES%d" % _t] = ("sbuf", [128, 64], "float32")
+    SCRATCH["UU%d" % _t] = ("sbuf", [128, 32], "float16")
     if _t:
-        SCRATCH["IB%d" % _t] = ("sbuf", [128, 2 * NC], "float16")
+        SCRATCH["BS%d" % _t] = ("sbuf", [128, NC], "float16")
         SCRATCH["NU%d" % _t] = ("sbuf", [128, 16], "uint16")
     if _t < ST - 1:
         SCRATCH["OL%d" % _t] = ("sbuf", [128, NC], "uint16")
-        SCRATCH["OB%d" % _t] = ("sbuf", [128, 2 * NC], "float16")
-        SCRATCH["RU%d" % _t] = ("sbuf", [128, 48], "uint16")
+        SCRATCH["OB%d" % _t] = ("sbuf", [128, NC], "float16")
+        SCRATCH["RU%d" % _t] = ("sbuf", [128, 32], "uint16")
 
-SEMAPHORES = ["sv", "ss", "sp", "sg", "dck", "dla", "dcu", "dgp", "loc", "ag1", "ag2", "dout", "dyc", "ayc"]
-for _t in (1, 2):
-    SEMAPHORES += ["ae%d" % _t, "an%d" % _t]
-    for _q in range(NQ):
-        SEMAPHORES += ["al%d_%d" % (_t, _q), "ab%d_%d" % (_t, _q)]
-SEMAPHORES += ["ay%d" % _q for _q in range(NQ)]
+SEMAPHORES = ["sv", "ss", "sp", "sg", "dla", "dcu", "dgp", "loc", "dout", "dyc", "ayc"]
+for _t in range(1, ST):
+    SEMAPHORES += ["au%d" % _t, "an%d" % _t, "ag%d" % _t, "ab%d_0" % _t, "ab%d_1" % _t] + ["al%d_%d" % (_t, _q) for _q in range(NQ)]
+SEMAPHORES += ["ay%d" % _q for _q in range(NQ)] + ["dck%d" % _q for _q in range(NQ)]
 
 
 def rank_program(g, core, T, topo):
@@ -97,39 +95,33 @@ def rank_program(g, core, T, topo):
         return
     A, COPY = AluOpType, ActivationFunctionType.Copy
     cores = list(T.cores)
-    n = len(cores)
-    nxt, nx2, prv, pv2 = cores[(rank + 1) % n], cores[(rank + 2) % n], cores[(rank - 1) % n], cores[(rank - 2) % n]
+    nr = len(cores)
+    ahead = {k: cores[(rank + k) % nr] for k in range(1 - ST, ST)}
+    nxt, prv = ahead[1], ahead[-1]
     V, S, P = g.vector, g.scalar, g.tensor
     que = {"v": V, "s": S, "p": P, "g": g, "y": g.sync}
     own = {"v": "sv", "s": "ss", "p": "sp", "g": "sg"}
     cnt = {"v": 0, "s": 0, "p": 0, "g": 0}
-    known, wr, rd, tot = {}, {}, {}, {"loc": 0}
+    known, wr, rd, bank, tot = {}, {}, {}, {}, {"loc": 0}
 
     def wait(q, sem, val):
         if known.get((q, sem), 0) < val:
             que[q].wait_ge(T.sem[sem], val)
             known[(q, sem)] = val
 
-    def deps(q, r, w):
-        need = {}
-        mine = own.get(q)
-        for k in r:
-            if k in wr:
-                sem, val = wr[k]
-                if not (q == "p" and sem == mine):
-                    need[sem] = max(need.get(sem, 0), val)
-        for k in w:
-            toks = dict(rd.get(k, {}))
-            toks.pop(mine, None)
-            if k in wr and not (q == "p" and wr[k][0] == mine):
-                toks[wr[k][0]] = max(toks.get(wr[k][0], 0), wr[k][1])
-            for sem, val in toks.items():
-                need[sem] = max(need.get(sem, 0), val)
+    def deps(q, r, w, b=()):
+        need, mine = {}, own.get(q)
+        toks = [wr[k] for k in list(r) + list(w) if k in wr]
+        toks += [(s, v) for k in w for s, v in rd.get(k, {}).items() if s != mine]
+        toks += [bank[k] for k in b if k in bank and bank[k][0] != mine]
+        for sem, val in toks:
+            need[sem] = max(need.get(sem, 0), val)
         for sem, val in need.items():
             wait(q, sem, val)
 
-    def op(q, fn, r=(), w=()):
-        deps(q, r, w)
+    def op(q, fn, r=(), w=(), b=()):
+        b = [("Q", k[1] % NQB) if k[0] == "Q" else k for k in b]
+        deps(q, r, w, b)
         fn().then_inc(T.sem[own[q]], 1)
         cnt[q] += 1
         for k in r:
@@ -137,6 +129,12 @@ def rank_program(g, core, T, topo):
         for k in w:
             wr[k] = (own[q], cnt[q])
             rd[k] = {}
+        for k in b:
+            bank[k] = (own[q], cnt[q])
+
+    def sums(b, terms):
+        for i, (o, l, x, r) in enumerate(terms):
+            op("p", lambda: P.matmul(o, l, x, i == 0, i == len(terms) - 1), r=r, b=[b])
 
     def load(q, out, in_, sem, key):
         que[q].dma_start(out, in_).then_inc(T.sem[sem], 16)
@@ -154,216 +152,243 @@ def rank_program(g, core, T, topo):
     def arr(name, k):
         return T["%s%d" % (name, k)]
 
+    CB = W // NQ
+    call = [("C", q) for q in range(NQ)]
     load("s", T.cui[:], T.cu[:], "dcu", "cui")
-    load("y", T.Cx[:, 0:W], T.ck[:], "dck", "C")
-    load("s", T.gapi[:], T.gap[:], "dgp", "gapi")
+    load("y", T.Cx[:, 0:CB], T.ck[:, 0:CB], "dck0", ("C", 0))
     load("y", T.Lt[:], T.la[:], "dla", "Lt")
+    for q in range(1, NQ):
+        load("y", T.Cx[:, CB * q:CB * q + CB], T.ck[:, CB * q:CB * q + CB], "dck%d" % q, ("C", q))
+    load("y", T.gapi[:], T.gap[:], "dgp", "gapi")
     for t in (1, 2):
-        lands(prv, "ae%d" % t, ("E", t))
+        lands(prv, "au%d" % t, ("UU", t, 0))
         lands(prv, "an%d" % t, ("NU", t))
         for q in range(NQ):
             lands(prv, "al%d_%d" % (t, q), ("LI", t, q))
-            lands(prv, "ab%d_%d" % (t, q), ("IB", t, q))
-    lands(prv, "ag1", ("GP", 1))
-    lands(pv2, "ag2", ("GP", 2))
+        lands(ahead[-t], "ag%d" % t, ("GP", t))
+        for h in range(2):
+            lands(prv, "ab%d_%d" % (t, h), ("BS", t, h))
 
-    op("g", lambda: g.iota(T.j8[:], [[0, 16]], 0, 8), w=["j8"])
-    op("g", lambda: g.iota(T.jq[:], [[128, 16]], 0, 0), w=["jq"])
+    def scaled(name, src, k):
+        op("s", lambda: S.activation(T[name][:], T[src][:], COPY, scale=k), r=[src], w=[name])
+
     op("v", lambda: V.memset(T.ones[:], 1.0), w=["ones"])
+    op("g", lambda: g.iota(T.j8[:], [[0, 16]], 0, 8), w=["j8"])
+    op("g", lambda: g.iota(T.jq[:, 0:16], [[0, 4], [128, 4]], 0, 0), w=[("jq", 0)])
+    op("g", lambda: g.iota(T.jq[:, 16:32], [[128, 16]], 0, 0), w=[("jq", 1)])
     op("g", lambda: g.affine_select(T.tI[:], T.ones[:], [[-1, 128]], A.is_equal, 0.0, 0, 1), r=["ones"], w=["tI"])
     op("g", lambda: g.affine_select(T.tC[:], T.ones[:], [[-16, 8], [0, 16]], A.is_ge, 0.0, 0, 1), r=["ones"], w=["tC"])
     op("g", lambda: g.affine_select(T.tB[:], T.tC[:], [[16, 8], [0, 16]], A.is_ge, 0.0, 15, -1), r=["tC"], w=["tB"])
-    op("g", lambda: g.iota(T.tj[:], [[0, 2], [-1, 128]], 128, 1), w=["tj"])
-    for h in range(2):
-        hs = slice(64 * h, 64 * h + 64)
-        op("g", lambda: g.affine_select(T.tD[:, hs], T.ones[:, hs], [[0, 4], [-16, 16]], A.is_ge, 0.0, 128 * h, 1), r=["ones"], w=[("tD", h)])
-        op("g", lambda: g.affine_select(T.tF[:, hs], T.tD[:, hs], [[0, 4], [16, 16]], A.is_ge, 0.0, 15 - 128 * h, -1), r=[("tD", h)], w=[("tF", h)])
+    op("g", lambda: g.iota(T.tj[:], [[-1, CH]], 128, 1), w=["tj"])
     op("v", lambda: V.memset(T.mask[:], 1.0), w=["mask"])
+    op("v", lambda: V.memset(T.oneb[:], 1.0), w=["oneb"])
     op("v", lambda: V.memset(T.mask[:, 0::16], 0.0), w=["mask"])
-    op("v", lambda: V.memset(T.CSh[:], -2.5 / 16), w=["CSh"])
     op("v", lambda: V.tensor_scalar(T.j8a[:], T.j8[:], 127, None, A.bitwise_and), r=["j8"], w=["j8a"])
-    op("v", lambda: V.tensor_tensor(T.i8[:], T.j8a[:], T.jq[:], A.add), r=["j8a", "jq"], w=["i8"])
-    op("v", lambda: V.tensor_scalar(T.ic[:], T.i8[:], 3, None, A.logical_shift_right), r=["i8"], w=["ic"])
-    op("v", lambda: V.tensor_scalar(T.E0[:, 0:16], T.ic[:], W, None, A.add), r=["ic"], w=[("E0", 4)])
-    op("v", lambda: V.tensor_scalar(T.E1[:, 0:16], T.ic[:], W, None, A.add), r=["ic"], w=["E1d"])
-    op("v", lambda: V.tensor_copy(T.IDh[:], T.tI[:]), r=["tI"], w=["IDh"])
-    op("v", lambda: V.tensor_scalar(T.NKh[:], T.tI[:], -float(W), None, A.mult), r=["tI"], w=["NKh"])
-    op("v", lambda: V.tensor_scalar(T.PKh[:], T.tI[:], float(W), None, A.mult), r=["tI"], w=["PKh"])
-    op("v", lambda: V.tensor_scalar(T.BGh[:], T.tB[:], KB, None, A.mult), r=["tB"], w=["BGh"])
-    op("v", lambda: V.tensor_scalar(T.NBh[:], T.tB[:], -KB, None, A.mult), r=["tB"], w=["NBh"])
-    for k in range(4):
-        op("v", lambda: V.tensor_scalar(T.cr[:, 16 * k:16 * k + 16], T.cui[:], k, None, A.add), r=["cui"], w=[("cr", k)])
-    op("v", lambda: V.tensor_scalar(T.cm[:], T.cr[:], 7, None, A.bitwise_and), r=[("cr", k) for k in range(4)], w=["cm"])
-    for k in range(4):
-        op("v", lambda: V.tensor_tensor(T.E0[:, 16 + 16 * k:32 + 16 * k], T.cm[:, 16 * k:16 * k + 16], T.i8[:], A.add),
-           r=["cm", "i8"], w=[("E0", k)])
-    op("v", lambda: V.tensor_copy(T.ou[:], T.E0[:, 16:48]), r=[("E0", 0), ("E0", 1)], w=["ou"])
-    op("v", lambda: V.tensor_copy(T.LI0[:], T.Cx[:, 0:W].indirect(T.ou[:, 0:16])), r=["C", "ou"],
-       w=[("LI", 0, q) for q in range(NQ)])
-    op("v", lambda: V.tensor_copy(T.I0[:], T.LI0[:]), r=[("LI", 0, q) for q in range(NQ)], w=[("IB", 0, q) for q in range(NQ)])
-    op("v", lambda: V.tensor_copy(T.GP0[:], T.gapi[:]), r=["gapi"], w=[("GP", 0)])
-    send(nxt, T.GP1[:], T.GP0[:], "ag1", [("GP", 0)])
-    send(nx2, T.GP2[:], T.GP0[:], "ag2", [("GP", 0)])
+    op("v", lambda: V.memset(T.R8b[0:1, 0:128], ULP8), w=["R8p"])
+    op("v", lambda: V.memset(T.R8b[0:1, 128:256], -ULP8), w=["R8n"])
+    for k in range(2):
+        op("v", lambda: V.tensor_tensor(T.i8[:, 16 * k:16 * k + 16], T.j8a[:], T.jq[:, 16 * k:16 * k + 16], A.add), r=["j8a", ("jq", k)], w=[("i8", k)])
+    op("v", lambda: V.tensor_scalar(T.ca[:], T.cui[:], 1, None, A.add), r=["cui"], w=["ca"])
+    op("v", lambda: V.tensor_tensor(T.cc[:, 0:16], T.cui[:], T.i8[:, 0:16], A.add), r=["cui", ("i8", 0)], w=[("cc", 0)])
+    op("v", lambda: V.tensor_scalar(T.cb[:], T.ca[:], 7, None, A.bitwise_and), r=["ca"], w=["cb"])
+    op("v", lambda: V.tensor_copy(T.UU0[:, 0:16], T.cui[:]), r=["cui"], w=[("UU", 0, 0)])
+    op("v", lambda: V.tensor_tensor(T.cc[:, 16:32], T.cb[:], T.i8[:, 16:32], A.add), r=["cb", ("i8", 1)], w=[("cc", 1)])
+    scaled("NKh", "tI", -float(W))
+    op("v", lambda: V.tensor_copy(T.ou[:], T.cc[:]), r=[("cc", 0), ("cc", 1)], w=["ou"])
+    for name, src, k in (("PKh", "tI", float(W)), ("IDh", "tI", 1.0), ("NIh", "tI", -1.0), ("IDb", "tI", 1.0),
+                         ("BGb", "tB", 1.0), ("PHb", "tB", HUGE), ("NHb", "tB", -HUGE)):
+        scaled(name, src, k)
     op("v", lambda: V.tensor_scalar(T.tk[:], T.tj[:], 15, None, A.bitwise_and), r=["tj"], w=["tk"])
-    op("v", lambda: V.tensor_scalar(T.te[:], T.tk[:], 0, None, A.is_equal), r=["tk"], w=["te"])
-    op("v", lambda: V.tensor_scalar(T.TH[:], T.te[:], -1048576.0, 1048576.0 + 2.5 * KB, A.mult, A.add), r=["te"], w=["TH"])
-    op("v", lambda: V.tensor_scalar(T.Bh[:], T.tF[:], BIG, None, A.mult), r=[("tF", 0), ("tF", 1)], w=["Bh"])
+    op("v", lambda: V.memset(T.K1[:, 0:16], 3.5), w=[("K1", 0)])
+    op("v", lambda: V.memset(T.K1[:, 16:32], 2.5), w=[("K1", 1)])
+    op("v", lambda: V.tensor_scalar(T.TH[:], T.tk[:], 1024.0, 2.5, A.mult, A.add), r=["tk"], w=["TH"])
+    op("v", lambda: V.tensor_scalar(T.K2[:, 0:16], T.i8[:, 16:32], float(W), None, A.add), r=[("i8", 1)], w=[("K2", 0)])
+    op("v", lambda: V.tensor_scalar(T.K2[:, 16:32], T.i8[:, 16:32], 1.0, None, A.add), r=[("i8", 1)], w=[("K2", 1)])
 
-    def cols(q):
-        return slice(CH * q, CH * q + CH)
+    def cols(q, a=0):
+        return slice(CH * q + a, CH * q + CH)
 
-    def iap(t, q):
-        return T.I0[:, cols(q)] if t == 0 else arr("IB", t)[:, 2 * CH * q:2 * CH * q + CH]
+    def two(q):
+        return slice(CH * q, CH * q + 2 * CH)
 
-    def bap(t, q):
-        return T.I0[:, cols(q)] if t == 0 else arr("IB", t)[:, 2 * CH * q + CH:2 * CH * q + 2 * CH]
+    def slot(q, k):
+        a = CH * (3 * (q // NQB) + k)
+        return arr("Q", q % NQB)[:, a:a + CH]
 
-    def a1(q):
-        return T.AB[:, 256 + CH * q:256 + CH * q + CH]
+    def ub(t, q):
+        return (NQ * t + q) % NUB
 
-    def Lg(t, q, b=0):
-        k = HV * b
-        op("s", lambda: S.activation(arr("X", q)[:, 16 * k:CW], T.Lt[:, 0:W].indirect(arr("LI", t)[:, CH * q + k:CH * q + CH]), COPY),
-           r=["Lt", ("LI", t, q)], w=[("X", q, 1)] if b else [("X", q, 0), ("X", q, 1)])
+    def Ig(t, q):
+        op("v", lambda: V.tensor_copy(T.LI0[:, cols(q)], T.Cx[:, CB * q:CB * q + CB].indirect(T.ou[:, 4 * q:4 * q + 4])),
+           r=[("C", q), "ou"], w=[("LI", 0, q)])
+
+    def Ih(t, q):
+        op("v", lambda: V.tensor_copy(arr("IH", t)[:, two(q)], arr("LI", t)[:, two(q)]), r=[("LI", t, q), ("LI", t, q + 1)], w=[("IH", t, q // 2)])
+
+    def Gp(t, q):
+        op("s", lambda: S.activation(T.GP0[:], T.gapi[:], COPY), r=["gapi"], w=[("GP", 0)])
+        for u in range(1, ST):
+            send(ahead[u], arr("GP", u)[:], T.GP0[:], "ag%d" % u, [("GP", 0)])
+
+    def Lg(t, q):
+        k = VL.get(NQ * t + q, 0)
+        op("s", lambda: S.activation(arr("X", q)[:, 16 * k:CW], T.Lt[:, 0:W].indirect(arr("LI", t)[:, cols(q, k)]), COPY),
+           r=["Lt", ("LI", t, q)], w=[("X", q, 1)] if k else [("X", q, 0), ("X", q, 1)])
 
     def Lv(t, q):
-        op("v", lambda: V.tensor_copy(arr("X", q)[:, 0:16 * HV], T.Lt[:, 0:W].indirect(arr("LI", t)[:, CH * q:CH * q + HV])),
-           r=["Lt", ("LI", t, q)], w=[("X", q, 0)])
+        k = VL.get(NQ * t + q, 0)
+        if k:
+            op("v", lambda: V.tensor_copy(arr("X", q)[:, 0:16 * k], T.Lt[:, 0:W].indirect(arr("LI", t)[:, CH * q:CH * q + k])),
+               r=["Lt", ("LI", t, q)], w=[("X", q, 0)])
 
     def Mx(t, q):
         op("v", lambda: V.tensor_tensor_scan(arr("R", q)[:], T.mask[:], arr("X", q)[:], 0.0, A.mult, A.max),
            r=["mask", ("X", q, 0), ("X", q, 1)], w=[("R", q)])
 
-    def Ug(t, q, b):
-        for k in range(8 * b, 8 * b + 8):
-            o, key = arr("U", q % 2)[:, CH * k:CH * k + CH], ("U", q % 2, b)
-            op("p", lambda: P.matmul(o, T.NKh[:], arr("X", q)[:, k::16], True, False), r=["NKh", ("X", q, 0), ("X", q, 1)], w=[key])
-            op("p", lambda: P.matmul(o, T.PKh[:], arr("R", q)[:, 15::16], False, True), r=["PKh", ("R", q)], w=[key])
+    def Ux(t, q):
+        for b in range(2):
+            op("p", lambda: P.matmul(arr("U", ub(t, q))[:, BANK * b:BANK * b + BANK], T.NKh[:], arr("X", q)[:, b::2], True, False),
+               r=["NKh", ("X", q, 0), ("X", q, 1)], b=[("U", ub(t, q), b)])
 
-    def Wm(t, q, b):
-        for k in range(8 * b, 8 * b + 8):
-            op("v", lambda: V.tensor_tensor(arr("Wm", q)[:, k::16], arr("X", q)[:, k::16], arr("U", q % 2)[:, CH * k:CH * k + CH], A.min),
-               r=[("X", q, 0), ("X", q, 1), ("U", q % 2, b)], w=[("Wm", q, k)])
+    def Um(b):
+        def part(t, q):
+            for k in range(8):
+                op("p", lambda: P.matmul(arr("U", ub(t, q))[:, BANK * b + k:BANK * b + BANK:8], T.PKh[:], arr("R", q)[:, 15::16], False, k == 7),
+                   r=["PKh", ("R", q)], b=[("U", ub(t, q), b)])
+        return part
+
+    def Wm(b):
+        def part(t, q):
+            op("v", lambda: V.tensor_tensor(arr("Wm", q)[:, b::2], arr("X", q)[:, b::2], arr("U", ub(t, q))[:, BANK * b:BANK * b + BANK], A.min),
+               r=[("X", q, 0), ("X", q, 1)], w=[("Wm", q, b)], b=[("U", ub(t, q), b)])
+        return part
 
     def Sc(t, q):
         op("v", lambda: V.tensor_tensor_scan(arr("S2", q)[:], T.mask[:], arr("Wm", q)[:], 0.0, A.mult, A.max),
-           r=["mask"] + [("Wm", q, k) for k in range(16)], w=[("S2", q)])
+           r=["mask", ("Wm", q, 0), ("Wm", q, 1)], w=[("S2", q, 0), ("S2", q, 1)])
 
     def Sk(t, q):
-        op("v", lambda: V.tensor_copy(T.SL[:, cols(q)], arr("S2", q)[:, 15::16]), r=[("S2", q)], w=[("SL", q)])
+        op("v", lambda: V.tensor_copy(T.SL[:, cols(q)], arr("S2", q)[:, 15::16]), r=[("S2", q, 0), ("S2", q, 1)], w=[("SL", q)])
 
     def Cg(t, q):
-        k = TV if (t, q) == (ST - 1, NQ - 1) else 0
-        op("s", lambda: S.activation(arr("Y", q)[:, 16 * k:CW], T.Cx[:, 0:W].indirect(T.SL[:, CH * q + k:CH * q + CH]), COPY),
-           r=["C", ("SL", q)], w=[("Y", q)])
+        k = VC.get(NQ * t + q, 0)
+        op("s", lambda: S.activation(arr("Y", q)[:, 16 * k:CW], T.Cx[:, 0:W].indirect(T.SL[:, cols(q, k)]), COPY),
+           r=call + [("SL", q)], w=[("Y", q, 1)] if k else [("Y", q, 0), ("Y", q, 1)])
 
     def Cv(t, q):
-        op("v", lambda: V.tensor_copy(arr("Y", q)[:, 0:16 * TV], T.Cx[:, 0:W].indirect(T.SL[:, CH * q:CH * q + TV])),
-           r=["C", ("SL", q)], w=[("Yv", q)])
+        k = VC.get(NQ * t + q, 0)
+        if k:
+            op("v", lambda: V.tensor_copy(arr("Y", q)[:, 0:16 * k], T.Cx[:, 0:W].indirect(T.SL[:, CH * q:CH * q + k])),
+               r=call + [("SL", q)], w=[("Y", q, 0)])
 
-    def Rl(t):
-        if t == 0:
-            op("v", lambda: V.tensor_copy(T.REL[:], T.Cx[:, 0:W].indirect(T.ou[:, 16:32])), r=["C", "ou"], w=["REL"])
-        else:
-            op("s", lambda: S.activation(T.REL[:], T.Cx[:, 0:W].indirect(arr("NU", t)[:]), COPY), r=["C", ("NU", t)], w=["REL"])
+    def Rl(t, q):
+        lst, key = (T.ou[:, 16:32], "ou") if t == 0 else (arr("NU", t)[:], ("NU", t))
+        op("s", lambda: S.activation(T.REL[:], T.Cx[:, 0:W].indirect(lst), COPY), r=call + [key], w=["REL"])
 
-    def PTI(t):
-        for q in range(NQ):
-            op("p", lambda: P.matmul(T.AB[:, cols(q)], T.IDh[:], iap(t, q), True, True), r=["IDh", ("IB", t, q)], w=["AB"])
-        for q in range(NQ):
-            op("p", lambda: P.matmul(T.TB[:, cols(q)], T.IDh[:], bap(t, q), True, False), r=["IDh", ("IB", t, q)], w=["TB"])
-            op("p", lambda: P.matmul(T.TB[:, cols(q)], T.IDh[:], arr("GP", t)[:, cols(q)], False, True), r=[("GP", t)], w=["TB"])
+    def pick(b, o, x, key, q):
+        rel, fd = T.REL[:, cols(q)], T.FD[:, cols(q)]
+        sums(b, [(o, T.IDh[:], x, [key]), (o, T.NIh[:], rel, ["NIh", "REL"]), (o, T.PHb[:], fd, ["PHb", ("FD", q)]), (o, T.NHb[:], fd, ["NHb"]),
+                 (o, T.IDh[:], rel, [])])
+
+    def base(t, q):
+        return (arr("BS", t)[:, cols(q)], ("BS", t, q // 2)) if t else (T.IH0[:, cols(q)], ("IH", 0, q // 2))
+
+    def PTI(t, q):
+        sums(("Q", q), [(slot(q, 0), T.IDh[:], arr("IH", t)[:, cols(q)], ["IDh", ("IH", t, q // 2)])])
+        x, key = base(t, q)
+        sums(("Q", q), [(slot(q, 1), T.IDh[:], x, [key]), (slot(q, 1), T.IDh[:], arr("GP", t)[:, cols(q)], [("GP", t)])])
 
     def Cm(t, q):
         op("v", lambda: V.tensor_tensor_scan(arr("R2", q)[:], T.mask[:], arr("Y", q)[:], 0.0, A.mult, A.max),
-           r=["mask", ("Y", q), ("Yv", q)], w=[("R2", q)])
+           r=["mask", ("Y", q, 0), ("Y", q, 1)], w=[("R2", q)])
 
     def Ge(t, q):
-        op("v", lambda: V.tensor_tensor(T.NEW[:, cols(q)], arr("R2", q)[:, 15::16], T.AB[:, cols(q)], A.max),
-           r=[("R2", q), "AB"], w=[("NEW", q)])
+        op("v", lambda: V.tensor_tensor(T.NEW[:, cols(q)], arr("R2", q)[:, 15::16], slot(q, 0), A.max),
+           r=[("R2", q)], w=[("NEW", q)], b=[("Q", q)])
 
     def Gb(t, q):
-        op("v", lambda: V.tensor_tensor(T.GE[:, cols(q)], T.NEW[:, cols(q)], T.TB[:, cols(q)], A.is_ge),
-           r=[("NEW", q), "TB"], w=[("GE", q)])
+        op("v", lambda: V.tensor_tensor(T.GE[:, cols(q)], T.NEW[:, cols(q)], slot(q, 1), A.is_ge),
+           r=[("NEW", q)], w=[("GE", q)], b=[("Q", q)])
 
     def Pb(t, q):
-        for k, m in ((0, "BGh"), (1, "NBh")):
-            op("p", lambda: P.matmul(T.BK[:, CH * k:CH * k + CH], T[m][:], T.CSh[:, 0:CH], True, False), r=[m, "CSh"], w=["BK"])
-            op("p", lambda: P.matmul(T.BK[:, CH * k:CH * k + CH], T[m][:], T.GE[:, cols(q)], False, True), r=[m, ("GE", q)], w=["BK"])
+        sums(("Q", q), [(slot(q, 2), T.BGb[:], T.GE[:, cols(q)], ["BGb", ("GE", q)])])
 
-    def Se(t, q):
-        op("v", lambda: V.tensor_tensor(a1(q), T.REL[:, cols(q)], T.BK[:, 0:CH], A.min), r=["REL", "BK", "AB"], w=[("a1", q)])
-        op("v", lambda: V.tensor_tensor(T.A2[:, cols(q)], T.NEW[:, cols(q)], T.BK[:, CH:2 * CH], A.min), r=[("NEW", q), "BK"], w=[("A2", q)])
+    def Fd(t, q):
+        op("v", lambda: V.tensor_tensor(T.FD[:, cols(q)], slot(q, 2), T.TH[:], A.is_ge), r=["TH"], w=[("FD", q)], b=[("Q", q)])
 
-    def Sh(t, q):
-        o = T.YO[:, cols(q)] if t == ST - 1 else arr("OB", t)[:, 2 * CH * q:2 * CH * q + CH]
-        op("v", lambda: V.tensor_tensor(o, T.A2[:, cols(q)], a1(q), A.max), r=[("A2", q), ("a1", q), "AB"], w=[("OBi", t, q)])
-        if t == ST - 1:
-            send(nxt, T.YL[:, cols(q)], T.YO[:, cols(q)], "ay%d" % q, [("OBi", t, q)])
+    def Pq(t, q):
+        pick(("Q", q), slot(q, 0), T.NEW[:, cols(q)], ("NEW", q), q)
+
+    def Po(t, q):
+        if t < ST - 1:
+            pick("Z", T.Z[:, cols(q)], *base(t, q), q)
+
+    def So(t, q):
+        if t < ST - 1:
+            if OV:
+                op("v", lambda: V.tensor_copy(arr("OB", t)[:, two(q)], T.Z[:, two(q)]), w=[("OB", t, q)], b=["Z"])
+            else:
+                op("s", lambda: S.activation(arr("OB", t)[:, two(q)], T.Z[:, two(q)], COPY), w=[("OB", t, q)], b=["Z"])
+            send(nxt, arr("BS", t + 1)[:, two(q)], arr("OB", t)[:, two(q)], "ab%d_%d" % (t + 1, q // 2), [("OB", t, q)])
 
     def Sj(t, q):
-        op("v", lambda: V.tensor_copy(arr("OL", t)[:, cols(q)], arr("OB", t)[:, 2 * CH * q:2 * CH * q + CH]), r=[("OBi", t, q)], w=[("OL", t, q)])
+        if t == ST - 1:
+            op("v", lambda: V.tensor_copy(T.YO[:, cols(q)], slot(q, 0)), w=[("YO", q)], b=[("Q", q)])
+            send(nxt, T.YL[:, cols(q)], T.YO[:, cols(q)], "ay%d" % q, [("YO", q)])
+            return
+        op("v", lambda: V.tensor_copy(arr("OL", t)[:, cols(q)], slot(q, 0)), w=[("OL", t, q)], b=[("Q", q)])
         send(nxt, arr("LI", t + 1)[:, cols(q)], arr("OL", t)[:, cols(q)], "al%d_%d" % (t + 1, q), [("OL", t, q)])
 
-    def Sf(t, q):
-        op("v", lambda: V.tensor_tensor(T.A3[:, cols(q)], bap(t, q), T.BK[:, CH:2 * CH], A.min), r=[("IB", t, q), "BK"], w=[("A3", q)])
+    ZU, ZL = NC, NC + 16
 
-    def Sb(t, q):
-        ob = arr("OB", t)[:, 2 * CH * q + CH:2 * CH * q + 2 * CH]
-        op("v", lambda: V.tensor_tensor(ob, T.A3[:, cols(q)], a1(q), A.max), r=[("A3", q), ("a1", q), "AB"], w=[("OBb", t, q)])
-        send(nxt, arr("IB", t + 1)[:, 2 * CH * q:2 * CH * (q + 1)], arr("OB", t)[:, 2 * CH * q:2 * CH * (q + 1)], "ab%d_%d" % (t + 1, q),
-             [("OBi", t, q), ("OBb", t, q)])
-
-    def Pl(t):
-        for h in range(2):
-            op("p", lambda: P.matmul(T.TB[:, 256 + 128 * h:384 + 128 * h], T.GE[:, 128 * h:128 * h + 128], T.BGh[:], True, True),
-               r=["BGh"] + [("GE", q) for q in range(NQ)], w=["TB"])
-
-    def Vl(t):
-        op("v", lambda: V.tensor_tensor(T.Ah[:], T.TB[:, 256:512], T.TH[:], A.is_ge), r=["TB", "TH"], w=["Ah"])
-
-    def Pd(t):
-        w = 16 * (4, 3, 1)[t]
-        for h in range(2):
-            op("p", lambda: P.matmul(T.BK[:, 128:128 + w], T.Ah[:, 128 * h:128 * h + 128], T.Bh[:, 64 * h:64 * h + w], h == 0, h == 1),
-               r=["Ah", "Bh"], w=["BK"])
-
-    def Sl(t):
-        w = 16 * (4, 3, 1)[t]
-        e = T.EC if t == ST - 1 else arr("E", t)
-        src = [("E0", k) for k in range(5)] if t == 0 else [("E", t), "E1d"] if t == 1 else ["EC0", "EC1"]
-        op("v", lambda: V.tensor_tensor(T.BK[:, 192:192 + w], e[:, 16:16 + w], T.BK[:, 128:128 + w], A.min), r=src + ["BK"], w=["lt1"])
-        op("v", lambda: V.tensor_tensor(T.lt2[:, 0:w], e[:, 0:w], T.BK[:, 128:128 + w], A.subtract), r=src + ["BK"], w=["lt2"])
-
-    def Sz(t):
-        w = 16 * (4, 3, 1)[t]
-        res = arr("RES", t)
-        op("v", lambda: V.tensor_tensor(res[:, 0:w], T.lt2[:, 0:w], T.BK[:, 192:192 + w], A.max), r=["lt1", "lt2", "BK"], w=[("RES", t)])
+    def Pu(t, q):
+        keys = [("FD", k) for k in range(NQ)]
         if t == ST - 1:
-            send(nxt, T.YCL[:], res[:, 0:16], "ayc", [("RES", t)])
+            op("v", lambda: V.tensor_tensor_scan(T.FL[:], T.mask[:, 0:NC], T.FD[:], 0.0, A.mult, A.max), r=keys, w=["FL"])
+            return
+        o = T.Z[:, ZU:ZU + 16]
+        sums("Z", [(o, T.IDh[:], arr("UU", t)[:, 0:16], [("UU", t, 0)])] + [(o, T.IDb[:], T.FD[:, a::16], ["IDb"] + keys) for a in range(16)])
 
-    def Sy(t):
-        res = arr("RES", t)
-        op("v", lambda: V.tensor_copy(arr("RU", t)[:], res[:, 0:48]), r=[("RES", t)], w=[("RU", t)])
-        send(nxt, arr("NU", t + 1)[:], arr("RU", t)[:, 32:48], "an%d" % (t + 1), [("RU", t)])
-        if t == 0:
-            send(nxt, T.E1[:, 16:64], res[:, 16:64], "ae1", [("RES", t)])
-        else:
-            send(nxt, T.E2[:, 0:32], res[:, 16:48], "ae2", [("RES", t)])
+    def Vu(t, q):
+        uu = arr("UU", t)
+        if t < ST - 1:
+            op("v", lambda: V.tensor_copy(uu[:, 16:32], T.Z[:, ZU:ZU + 16]), w=[("UU", t, 1)], b=["Z"])
+            send(nxt, arr("UU", t + 1)[:, 0:16], uu[:, 16:32], "au%d" % (t + 1), [("UU", t, 1)])
 
-    def Scat(t):
-        op("v", lambda: V.tensor_copy(T.Cx[:, 0:W + NC].indirect(arr("RU", t)[:, 0:16]), T.NEW[:]),
-           r=[("RU", t)] + [("NEW", q) for q in range(NQ)], w=["C"])
+    def Pw(t, q):
+        uu, last = arr("UU", t), t == ST - 1
+        w = 16 if last else 32
+        o = T.Z[:, ZL:ZL + w]
+        xs = [(uu[:, 0:16], [("UU", t, 0)]), (T.FL[:, 15::16], ["FL"])] if last else [(uu[:], [("UU", t, 0), ("UU", t, 1)])]
+        terms = [(o, T.IDh[:], T.K1[:, 0:w], [("K1", 0), ("K1", 1)])] + [(o, T.NIh[:], x, keys) for x, keys in xs]
+        terms += [(o, T.R8b[0:1, 0:128], T.oneb[0:1, 0:w], ["R8p", "oneb"]), (o, T.R8b[0:1, 128:256], T.oneb[0:1, 0:w], ["R8n"])]
+        terms += [(o, T.IDh[:], x, []) for x, keys in xs]
+        if not last:
+            o1 = T.Z[:, ZL:ZL + 16]
+            terms += [(o1, T.PKh[:], uu[:, 0:16], []), (o1, T.NKh[:], uu[:, 16:32], []), (o, T.IDh[:], T.K2[:], [("K2", 0), ("K2", 1)])]
+        sums("Z", terms)
 
-    def Ec(t):
-        for k in range(2):
-            op("v", lambda: V.tensor_tensor(T.EC[:, 16 * k:16 * k + 16], T.E2[:, 16 * k:16 * k + 16], T.i8[:], A.subtract),
-               r=[("E", 2), "i8"], w=["EC%d" % k])
+    def Vy(t, q):
+        if t == ST - 1:
+            op("v", lambda: V.tensor_copy(T.YC[:], T.Z[:, ZL:ZL + 16]), w=["YC"], b=["Z"])
+            send(nxt, T.YCL[:], T.YC[:], "ayc", ["YC"])
+            return
+        op("v", lambda: V.tensor_copy(arr("RU", t)[:], T.Z[:, ZL:ZL + 32]), w=[("RU", t)], b=["Z"])
+        send(nxt, arr("NU", t + 1)[:], arr("RU", t)[:, 16:32], "an%d" % (t + 1), [("RU", t)])
 
-    parts = {"L": Lg, "l": Lv, "M": Mx, "U": Ug, "W": Wm, "S": Sc, "k": Sk, "C": Cg, "c": Cv, "R": Rl, "P": PTI, "m": Cm, "G": Ge, "g": Gb,
-             "B": Pb, "E": Se, "H": Sh, "J": Sj, "F": Sf, "K": Sb, "p": Pl, "v": Vl, "d": Pd, "s": Sl, "z": Sz, "y": Sy, "x": Scat, "e": Ec}
-    for tok in SCHED.split():
-        parts[tok[0]](*[int(c) for c in tok[1:]])
+    def Scat(t, q):
+        if t < ST - 1:
+            op("v", lambda: V.tensor_copy(T.Cx[:].indirect(arr("RU", t)[:, 0:16]), T.NEW[:]),
+               r=[("RU", t)] + [("NEW", k) for k in range(NQ)], w=call)
+
+    parts = {"I": Ig, "i": Ih, "A": Gp, "L": Lg, "l": Lv, "M": Mx, "X": Ux, "U": Um(0), "V": Um(1), "W": Wm(0), "Z": Wm(1),
+             "S": Sc, "k": Sk, "C": Cg, "c": Cv, "R": Rl, "P": PTI,
+             "m": Cm, "G": Ge, "g": Gb, "B": Pb, "f": Fd, "Q": Pq, "J": Sj, "o": Po, "O": So, "u": Pu, "v": Vu, "w": Pw, "y": Vy, "x": Scat}
+    for t, order in [(0, START)] + [(t, STEP) for t in range(ST - 1)] + [(ST - 1, LAST)]:
+        for tok in order.split():
+            n = NQ * t + int(tok[1:])
+            if n < NN:
+                parts[tok[0]](n // NQ, n % NQ)
 
     for q in range(NQ):
         wait("y", "ay%d" % q, len(topo.engines(prv, core)))

@@ -1,3 +1,4 @@
+from concourse.bass import DstId, RemoteDMATransfer
 from concourse.mybir import dt, AluOpType, ActivationFunctionType
 
 NQ, CH, ST, W = 4, 64, 3, 2048
@@ -7,16 +8,28 @@ NN = NQ * ST
 BANK = 512
 NUB = 2
 NQB = 7 - 2 * NUB
-OV = False
+CM = 64
+AT, AU = [0, CH, 4 * CH, 5 * CH], 8 * CH
+GAPAT = 4
+MERGE = 0
+OUTS = [0, 1, 2, 3, 4]
+LCUT = [0, 64, 128, 192, 256]
+CUT = [[0, 64, 128, 192, 256]] * (ST - 1) + [LCUT]
+TR = {10}
+WHO = dict({k: "g" for k in "A0 k4 k5 k6 k8 k9 k10 i0 i2 i4 i6 i8 i10".split()}, **{k: "s" for k in "J8 J9".split()})
 HUGE = 2.0 ** 40
 ULP8 = 1.5 * 2.0 ** 26
-VL = {0: 32, 1: 16}
-VC = {3: 32, 7: 32, 11: 8}
-START = "I0 L0 l0 I1 M0 X0 U0 V0 L1 l1 A0 X1 i0 I2 L2 W0 Z0 M1 S0 I3 k0 U1 V1"
-STEP = ("C0 L3 R0 W1 Z1 M2 S1 m0 P1 P0 X2 U2 V2 i2 k1 G0 W2 C1 g0 Z2 B0 f0 Q0 S2 J0 M3 k2 C2 L4 P2 X3 U3 V3 m1 W3 G1 Z3 g1 m2 B1 o0 f1 G2 "
-        "S3 g2 Q1 B2 o1 P3 J1 k3 f2 Q2 O0 C3 L5 c3 M4 J2 X4 o2 V4 U4 m3 G3 g3 W4 B3 f3 Z4 Q3 u0 J3 S4 v0 M5 w0 X5 y0 k4 x0 i4 o3 U5 V5 L6 O2")
-LAST = ("W1 M2 P0 X2 U2 L3 i2 Z1 W2 V2 Z2 S1 C0 M3 X3 S2 k1 V3 P2 U3 P1 m0 Z3 G0 k2 R0 C1 W3 C2 g0 B0 S3 f0 Q0 m1 k3 G1 J0 g1 m2 B1 f1 Q1 "
-        "P3 G2 g2 c3 J1 B2 f2 C3 m3 Q2 G3 J2 g3 B3 f3 Q3 J3 u0 w0 y0")
+VL = {0: 32, 1: 16, 4: 8, 5: 16, 8: 8, 9: 16}
+VC = {3: 16, 7: 16, 11: 24}
+ORDER = """
+I0 L0 l0 I1 L1 X0 Y0 M0 V0 U0 l1 I2 Z0 W0 M1 i0 S0 I3 A0 k0 X1 Y1 V1 U1 L2 L3 C0 Z1 W1 M2 S1 M3 X2 Y2 U2 P1 V2 Y3 X3 U3 P0 V3 k1 W2
+Z2 m0 S2 i2 G0 W3 k2 g0 Z3 R0 C1 C2 B0 f0 Q0 m1 J0 S3 G1 k3 g1 C3 m2 P3 B1 P2 f1 Q1 o1 G2 c3 g2 B2 o0 J1 m3 f2 L4 L5 O0 G3 Q2 l4 g3
+J2 o2 X4 B3 Y4 M4 f3 l5 U4 V4 Q3 W4 J3 Z4 u0 v0 Y5 w0 o3 M5 S4 V5 X5 U5 y0 O2 L6 z0 k4 x0 i4 L7 C4 Z5 W5 M6 S5 M7 X6 Y6 U6 P5 V6 Y7
+X7 U7 P4 V7 k5 W6 Z6 m4 S6 i6 G4 W7 k6 g4 Z7 R4 C5 C6 B4 f4 Q4 m5 J4 S7 G5 k7 g5 C7 m6 P7 B5 P6 f5 Q5 o5 G6 c7 g6 B6 o4 J5 m7 f6 L8
+L9 O4 G7 Q6 l8 g7 J6 o6 X8 B7 Y8 M8 f7 l9 U8 V8 Q7 W8 J7 Z8 u4 v4 Y9 w4 o7 M9 S8 V9 X9 U9 y4 O6 L10 K10 z4 k8 x4 i8 L11 C8 Y10 X10
+M10 Z9 U10 E10 W9 N10 S9 M11 W10 m8 V10 F10 X11 U11 P8 Y11 V11 R8 k9 Z10 G8 C9 W11 g8 Z11 m9 P9 B8 S11 G9 k11 g9 k10 C10 f8 i10 c11
+C11 P10 Q8 B9 P11 m10 J8 f9 Q9 m11 G10 G11 J9 g10 B10 g11 f10 B11 f11 u8 Q10 Q11 J10 w8 J11 y8 z8
+"""
 
 SCRATCH = {
     "Lt": ("sbuf", [128, W], "int32"),
@@ -27,7 +40,7 @@ SCRATCH = {
     "tI": ("sbuf", [128, 128], "float32"),
     "tB": ("sbuf", [128, 128], "float32"),
     "tC": ("sbuf", [128, 128], "float32"),
-    "mask": ("sbuf", [128, CW], "float16"),
+    "mask": ("sbuf", [128, 16 * CM], "float16"),
     "IDh": ("sbuf", [128, 128], "float16"),
     "NIh": ("sbuf", [128, 128], "float16"),
     "NKh": ("sbuf", [128, 128], "float16"),
@@ -37,12 +50,14 @@ SCRATCH = {
     "PHb": ("sbuf", [128, 128], "bfloat16"),
     "NHb": ("sbuf", [128, 128], "bfloat16"),
     "R8b": ("sbuf", [128, 256], "bfloat16"),
-    "oneb": ("sbuf", [128, 32], "bfloat16"),
+    "R4b": ("sbuf", [128, 256], "bfloat16"),
+    "drop": ("sbuf", [128, BANK], "float16"),
+    "oneb": ("sbuf", [128, BANK], "bfloat16"),
     "K1": ("sbuf", [128, 32], "float16"),
     "K2": ("sbuf", [128, 32], "float16"),
-    "TH": ("sbuf", [128, CH], "float32"),
-    "tj": ("sbuf", [128, CH], "int32"),
-    "tk": ("sbuf", [128, CH], "int32"),
+    "TH": ("sbuf", [128, CM], "float32"),
+    "tj": ("sbuf", [128, CM], "int32"),
+    "tk": ("sbuf", [128, CM], "int32"),
     "j8": ("sbuf", [128, 16], "int32"),
     "jq": ("sbuf", [128, 32], "int32"),
     "j8a": ("sbuf", [128, 16], "int32"),
@@ -56,10 +71,8 @@ SCRATCH = {
     "GE": ("sbuf", [128, NC], "bfloat16"),
     "FL": ("sbuf", [128, NC], "float16"),
     "REL": ("sbuf", [128, NC], "float16"),
-    "YO": ("sbuf", [128, NC], "float32"),
-    "YL": ("sbuf", [128, NC], "float32"),
-    "YC": ("sbuf", [128, 16], "float32"),
-    "YCL": ("sbuf", [128, 16], "float32"),
+    "YO": ("sbuf", [128, NC + 16], "float32"),
+    "YL": ("sbuf", [128, NC + 16], "float32"),
     "FD": ("sbuf", [128, NC], "bfloat16"),
     "Z": ("psum", [128, BANK], "float32"),
 }
@@ -69,23 +82,17 @@ for _q in range(NQB):
     SCRATCH["Q%d" % _q] = ("psum", [128, BANK], "float32")
 for _q in range(NQ):
     for _n in ("X", "R", "Wm", "S2", "Y", "R2"):
-        SCRATCH["%s%d" % (_n, _q)] = ("sbuf", [128, CW], "float16")
+        SCRATCH["%s%d" % (_n, _q)] = ("sbuf", [128, 16 * CM if _n in ("Y", "R2") else CW], "float16")
 for _t in range(ST):
-    SCRATCH["LI%d" % _t] = ("sbuf", [128, NC], "uint16")
-    SCRATCH["IH%d" % _t] = ("sbuf", [128, NC], "float16")
+    SCRATCH["LI%d" % _t] = ("sbuf", [128, AU + 48], "uint16")
+    SCRATCH["IH%d" % _t] = ("sbuf", [128, AU + 32], "float16")
     SCRATCH["GP%d" % _t] = ("sbuf", [128, NC], "float16")
-    SCRATCH["UU%d" % _t] = ("sbuf", [128, 32], "float16")
-    if _t:
-        SCRATCH["BS%d" % _t] = ("sbuf", [128, NC], "float16")
-        SCRATCH["NU%d" % _t] = ("sbuf", [128, 16], "uint16")
     if _t < ST - 1:
-        SCRATCH["OL%d" % _t] = ("sbuf", [128, NC], "uint16")
-        SCRATCH["OB%d" % _t] = ("sbuf", [128, NC], "float16")
-        SCRATCH["RU%d" % _t] = ("sbuf", [128, 32], "uint16")
+        SCRATCH["OL%d" % _t] = ("sbuf", [128, AU + 48], "uint16")
 
-SEMAPHORES = ["sv", "ss", "sp", "sg", "dla", "dcu", "dgp", "loc", "dout", "dyc", "ayc"]
+SEMAPHORES = ["sv", "ss", "sp", "sg", "dla", "dcu", "dgp", "loc", "dout", "dyc"]
 for _t in range(1, ST):
-    SEMAPHORES += ["au%d" % _t, "an%d" % _t, "ag%d" % _t, "ab%d_0" % _t, "ab%d_1" % _t] + ["al%d_%d" % (_t, _q) for _q in range(NQ)]
+    SEMAPHORES += ["at%d" % _t, "ag%d" % _t] + ["al%d_%d" % (_t, _q) for _q in range(NQ)]
 SEMAPHORES += ["ay%d" % _q for _q in range(NQ)] + ["dck%d" % _q for _q in range(NQ)]
 
 
@@ -102,12 +109,13 @@ def rank_program(g, core, T, topo):
     que = {"v": V, "s": S, "p": P, "g": g, "y": g.sync}
     own = {"v": "sv", "s": "ss", "p": "sp", "g": "sg"}
     cnt = {"v": 0, "s": 0, "p": 0, "g": 0}
-    known, wr, rd, bank, tot = {}, {}, {}, {}, {"loc": 0}
+    known, seen, wr, rd, bank, tot = {q: {} for q in que}, {}, {}, {}, {}, {"loc": 0}
 
     def wait(q, sem, val):
-        if known.get((q, sem), 0) < val:
+        if known[q].get(sem, 0) < val:
             que[q].wait_ge(T.sem[sem], val)
-            known[(q, sem)] = val
+            for s, v in list(seen.get((sem, val), {}).items()) + [(sem, val)]:
+                known[q][s] = max(known[q].get(s, 0), v)
 
     def deps(q, r, w, b=()):
         need, mine = {}, own.get(q)
@@ -116,7 +124,7 @@ def rank_program(g, core, T, topo):
         toks += [bank[k] for k in b if k in bank and bank[k][0] != mine]
         for sem, val in toks:
             need[sem] = max(need.get(sem, 0), val)
-        for sem, val in need.items():
+        for sem, val in sorted(need.items(), key=lambda x: -sum(seen.get(x, {}).get(s, 0) >= v for s, v in need.items())):
             wait(q, sem, val)
 
     def op(q, fn, r=(), w=(), b=()):
@@ -124,6 +132,7 @@ def rank_program(g, core, T, topo):
         deps(q, r, w, b)
         fn().then_inc(T.sem[own[q]], 1)
         cnt[q] += 1
+        seen[(own[q], cnt[q])] = dict(known[q])
         for k in r:
             rd.setdefault(k, {})[own[q]] = cnt[q]
         for k in w:
@@ -136,6 +145,12 @@ def rank_program(g, core, T, topo):
         for i, (o, l, x, r) in enumerate(terms):
             op("p", lambda: P.matmul(o, l, x, i == 0, i == len(terms) - 1), r=r, b=[b])
 
+    def copy(part, t, q, out, in_, r, w, b=()):
+        who = WHO.get("%s%d" % (part, NQ * t + q), "v")
+        call = {"v": lambda: V.tensor_copy(out, in_), "s": lambda: S.activation(out, in_, COPY),
+                "g": lambda: g.affine_select(out, in_, [[0, out.shape[1]]], A.is_ge, 0.0, 0, 0)}
+        op(who, call[who], r, w, b)
+
     def load(q, out, in_, sem, key):
         que[q].dma_start(out, in_).then_inc(T.sem[sem], 16)
         wr[key] = (sem, 16)
@@ -146,8 +161,24 @@ def rank_program(g, core, T, topo):
         g.remote_dma(out, in_, T.sem[sem], T.sem.loc, pid, rid, topo.mask(core, dst))
         tot["loc"] += len(topo.engines(core, dst))
 
-    def lands(src, sem, key):
-        wr[key] = (sem, len(topo.engines(src, core)))
+    def apart(r):
+        src = cores[r % nr]
+        near, far = topo.engines(src, cores[(r + 1) % nr]), topo.engines(src, cores[(r + 2) % nr])
+        rest = [e for e in near if e not in far]
+        return (rest, far) if rest else (near[:len(near) // 2], far[len(far) // 2:])
+
+    def send2(out1, out2, in_, sem1, sem2, r):
+        deps("g", r, ())
+        moves = []
+        for k, out, sem, eng in zip((1, 2), (out1, out2), (sem1, sem2), apart(rank)):
+            rid, pid, _ = topo.addr(ahead[k])
+            moves.append(RemoteDMATransfer(dst_ids=[DstId(rid=rid, pnc=pid)], dma_engine_mask=sum(1 << e for e in eng),
+                                           remote_sem=T.sem[sem], src=in_, dst=out))
+            tot["loc"] += len(eng)
+        g.remote_dma_fused(moves, local_sem=T.sem.loc)
+
+    def lands(src, sem, key, count=None):
+        wr[key] = (sem, count or len(topo.engines(src, core)))
 
     def arr(name, k):
         return T["%s%d" % (name, k)]
@@ -157,29 +188,31 @@ def rank_program(g, core, T, topo):
     load("s", T.cui[:], T.cu[:], "dcu", "cui")
     load("y", T.Cx[:, 0:CB], T.ck[:, 0:CB], "dck0", ("C", 0))
     load("y", T.Lt[:], T.la[:], "dla", "Lt")
-    for q in range(1, NQ):
-        load("y", T.Cx[:, CB * q:CB * q + CB], T.ck[:, CB * q:CB * q + CB], "dck%d" % q, ("C", q))
-    load("y", T.gapi[:], T.gap[:], "dgp", "gapi")
+    for q in range(1, NQ + 1):
+        if q == GAPAT:
+            load("y", T.gapi[:], T.gap[:], "dgp", "gapi")
+        if q < NQ:
+            load("y", T.Cx[:, CB * q:CB * q + CB], T.ck[:, CB * q:CB * q + CB], "dck%d" % q, ("C", q))
     for t in (1, 2):
-        lands(prv, "au%d" % t, ("UU", t, 0))
-        lands(prv, "an%d" % t, ("NU", t))
+        lands(prv, "at%d" % t, ("LT", t))
         for q in range(NQ):
             lands(prv, "al%d_%d" % (t, q), ("LI", t, q))
-        lands(ahead[-t], "ag%d" % t, ("GP", t))
-        for h in range(2):
-            lands(prv, "ab%d_%d" % (t, h), ("BS", t, h))
+        lands(ahead[-t], "ag%d" % t, ("GP", t), len(apart(rank - t)[t - 1]))
 
     def scaled(name, src, k):
-        op("s", lambda: S.activation(T[name][:], T[src][:], COPY, scale=k), r=[src], w=[name])
+        if name in ("IDb", "NIh", "PHb"):
+            op("s", lambda: S.activation(T[name][:], T[src][:], COPY, scale=k), r=[src], w=[name])
+        else:
+            op("v", lambda: V.tensor_scalar(T[name][:], T[src][:], k, None, A.mult), r=[src], w=[name])
 
     op("v", lambda: V.memset(T.ones[:], 1.0), w=["ones"])
     op("g", lambda: g.iota(T.j8[:], [[0, 16]], 0, 8), w=["j8"])
     op("g", lambda: g.iota(T.jq[:, 0:16], [[0, 4], [128, 4]], 0, 0), w=[("jq", 0)])
     op("g", lambda: g.iota(T.jq[:, 16:32], [[128, 16]], 0, 0), w=[("jq", 1)])
+    op("g", lambda: g.iota(T.tj[:], [[-1, CM]], 128, 1), w=["tj"])
     op("g", lambda: g.affine_select(T.tI[:], T.ones[:], [[-1, 128]], A.is_equal, 0.0, 0, 1), r=["ones"], w=["tI"])
     op("g", lambda: g.affine_select(T.tC[:], T.ones[:], [[-16, 8], [0, 16]], A.is_ge, 0.0, 0, 1), r=["ones"], w=["tC"])
     op("g", lambda: g.affine_select(T.tB[:], T.tC[:], [[16, 8], [0, 16]], A.is_ge, 0.0, 15, -1), r=["tC"], w=["tB"])
-    op("g", lambda: g.iota(T.tj[:], [[-1, CH]], 128, 1), w=["tj"])
     op("v", lambda: V.memset(T.mask[:], 1.0), w=["mask"])
     op("v", lambda: V.memset(T.oneb[:], 1.0), w=["oneb"])
     op("v", lambda: V.memset(T.mask[:, 0::16], 0.0), w=["mask"])
@@ -191,13 +224,18 @@ def rank_program(g, core, T, topo):
     op("v", lambda: V.tensor_scalar(T.ca[:], T.cui[:], 1, None, A.add), r=["cui"], w=["ca"])
     op("v", lambda: V.tensor_tensor(T.cc[:, 0:16], T.cui[:], T.i8[:, 0:16], A.add), r=["cui", ("i8", 0)], w=[("cc", 0)])
     op("v", lambda: V.tensor_scalar(T.cb[:], T.ca[:], 7, None, A.bitwise_and), r=["ca"], w=["cb"])
-    op("v", lambda: V.tensor_copy(T.UU0[:, 0:16], T.cui[:]), r=["cui"], w=[("UU", 0, 0)])
+    op("v", lambda: V.tensor_copy(T.IH0[:, AU:AU + 16], T.cui[:]), r=["cui"], w=["u0"])
     op("v", lambda: V.tensor_tensor(T.cc[:, 16:32], T.cb[:], T.i8[:, 16:32], A.add), r=["cb", ("i8", 1)], w=[("cc", 1)])
     scaled("NKh", "tI", -float(W))
     op("v", lambda: V.tensor_copy(T.ou[:], T.cc[:]), r=[("cc", 0), ("cc", 1)], w=["ou"])
     for name, src, k in (("PKh", "tI", float(W)), ("IDh", "tI", 1.0), ("NIh", "tI", -1.0), ("IDb", "tI", 1.0),
                          ("BGb", "tB", 1.0), ("PHb", "tB", HUGE), ("NHb", "tB", -HUGE)):
         scaled(name, src, k)
+    op("s", lambda: S.activation(T.drop[:], T.mask[:, 1:BANK + 1], COPY, bias=-float(W), scale=float(W)), r=["mask"], w=["drop"])
+    op("v", lambda: V.memset(T.R4b[0:64, :], 0.0), w=["R4b"])
+    for row, val in ((0, 4096.0), (32, 1.5 * 2.0 ** 35)):
+        for k in range(2):
+            op("v", lambda: V.memset(T.R4b[row:row + 1, 128 * k:128 * k + 128], (1 - 2 * k) * val), r=["R4b"], w=[("R4b", row, k)])
     op("v", lambda: V.tensor_scalar(T.tk[:], T.tj[:], 15, None, A.bitwise_and), r=["tj"], w=["tk"])
     op("v", lambda: V.memset(T.K1[:, 0:16], 3.5), w=[("K1", 0)])
     op("v", lambda: V.memset(T.K1[:, 16:32], 2.5), w=[("K1", 1)])
@@ -208,138 +246,193 @@ def rank_program(g, core, T, topo):
     def cols(q, a=0):
         return slice(CH * q + a, CH * q + CH)
 
-    def two(q):
-        return slice(CH * q, CH * q + 2 * CH)
+    def at(q, a=0):
+        return slice(AT[q] + a, AT[q] + a + CH)
 
-    def slot(q, k):
-        a = CH * (3 * (q // NQB) + k)
-        return arr("Q", q % NQB)[:, a:a + CH]
+    def lk(t, q):
+        return ("LT", t) if MERGE and t and q == NQ - 1 else ("LI", t, q)
+
+    def cut(t, q):
+        return slice(CUT[t][q], CUT[t][q + 1])
+
+    def wid(t, q):
+        return CUT[t][q + 1] - CUT[t][q]
+
+    def slot(t, q, k):
+        a = 3 * CM * (q // NQB) + wid(t, q) * k
+        return arr("Q", q % NQB)[:, a:a + wid(t, q)]
 
     def ub(t, q):
         return (NQ * t + q) % NUB
 
     def Ig(t, q):
-        op("v", lambda: V.tensor_copy(T.LI0[:, cols(q)], T.Cx[:, CB * q:CB * q + CB].indirect(T.ou[:, 4 * q:4 * q + 4])),
+        op("v", lambda: V.tensor_copy(T.LI0[:, at(q)], T.Cx[:, CB * q:CB * q + CB].indirect(T.ou[:, 4 * q:4 * q + 4])),
            r=[("C", q), "ou"], w=[("LI", 0, q)])
 
     def Ih(t, q):
-        op("v", lambda: V.tensor_copy(arr("IH", t)[:, two(q)], arr("LI", t)[:, two(q)]), r=[("LI", t, q), ("LI", t, q + 1)], w=[("IH", t, q // 2)])
+        part = slice(AT[q], AT[q] + 2 * CH if t == 0 else AU + 16 if q else AT[2])
+        keys = [lk(t, q), lk(t, q + 1)] + ([] if t == 0 else [("LT", t)] if q else [("LI", t, 2)])
+        copy("i", t, q, arr("IH", t)[:, part], arr("LI", t)[:, part], keys, [("IH", t, q // 2)])
 
     def Gp(t, q):
-        op("s", lambda: S.activation(T.GP0[:], T.gapi[:], COPY), r=["gapi"], w=[("GP", 0)])
-        for u in range(1, ST):
-            send(ahead[u], arr("GP", u)[:], T.GP0[:], "ag%d" % u, [("GP", 0)])
+        copy("A", t, q, T.GP0[:], T.gapi[:], ["gapi"], [("GP", 0)])
+        send2(T.GP1[:], T.GP2[:], T.GP0[:], "ag1", "ag2", [("GP", 0)])
 
     def Lg(t, q):
-        k = VL.get(NQ * t + q, 0)
-        op("s", lambda: S.activation(arr("X", q)[:, 16 * k:CW], T.Lt[:, 0:W].indirect(arr("LI", t)[:, cols(q, k)]), COPY),
-           r=["Lt", ("LI", t, q)], w=[("X", q, 1)] if k else [("X", q, 0), ("X", q, 1)])
+        k, e = VL.get(NQ * t + q, 0), CH // 2 if NQ * t + q in TR else CH
+        if k < e:
+            op("s", lambda: S.activation(arr("X", q)[:, 16 * k:16 * e], T.Lt[:, 0:W].indirect(arr("LI", t)[:, AT[q] + k:AT[q] + e]), COPY),
+               r=["Lt", lk(t, q)], w=[("X", q, j) for j in range(1 if k else 0, 2 if e < CH else 3)])
+
+    def Lh(t, q):
+        if NQ * t + q in TR:
+            op("s", lambda: S.activation(arr("X", q)[:, BANK:CW], T.Lt[:, 0:W].indirect(arr("LI", t)[:, AT[q] + CH // 2:AT[q] + CH]), COPY),
+               r=["Lt", lk(t, q)], w=[("X", q, 2)])
 
     def Lv(t, q):
         k = VL.get(NQ * t + q, 0)
         if k:
-            op("v", lambda: V.tensor_copy(arr("X", q)[:, 0:16 * k], T.Lt[:, 0:W].indirect(arr("LI", t)[:, CH * q:CH * q + k])),
-               r=["Lt", ("LI", t, q)], w=[("X", q, 0)])
+            op("v", lambda: V.tensor_copy(arr("X", q)[:, 0:16 * k], T.Lt[:, 0:W].indirect(arr("LI", t)[:, AT[q]:AT[q] + k])),
+               r=["Lt", lk(t, q)], w=[("X", q, 0)])
 
-    def Mx(t, q):
-        op("v", lambda: V.tensor_tensor_scan(arr("R", q)[:], T.mask[:], arr("X", q)[:], 0.0, A.mult, A.max),
-           r=["mask", ("X", q, 0), ("X", q, 1)], w=[("R", q)])
+    def xk(t, q, b):
+        return [("X", q, j) for j in (((0, 1), (2,))[b] if NQ * t + q in TR else (0, 1, 2))]
 
-    def Ux(t, q):
-        for b in range(2):
-            op("p", lambda: P.matmul(arr("U", ub(t, q))[:, BANK * b:BANK * b + BANK], T.NKh[:], arr("X", q)[:, b::2], True, False),
-               r=["NKh", ("X", q, 0), ("X", q, 1)], b=[("U", ub(t, q), b)])
+    def Mx(b):
+        def part(t, q):
+            half = slice(BANK * b, BANK * b + BANK)
+            if NQ * t + q in TR:
+                op("v", lambda: V.tensor_tensor_scan(arr("R", q)[:, half], arr("X", q)[:, half], T.drop[:], 0.0, A.max, A.add),
+                   r=["drop"] + xk(t, q, b), w=[("R", q, b)])
+            elif b == 0:
+                op("v", lambda: V.tensor_tensor_scan(arr("R", q)[:], T.mask[:, 0:CW], arr("X", q)[:], 0.0, A.mult, A.max),
+                   r=["mask"] + xk(t, q, b), w=[("R", q, 0), ("R", q, 1)])
+        return part
+
+    def Ux(b):
+        def part(t, q):
+            half = slice(BANK * b, BANK * b + BANK)
+            m, x = ("NIh", arr("X", q)[:, half]) if NQ * t + q in TR else ("NKh", arr("X", q)[:, b::2])
+            op("p", lambda: P.matmul(arr("U", ub(t, q))[:, half], T[m][:], x, True, False), r=[m] + xk(t, q, b), b=[("U", ub(t, q), b)])
+        return part
 
     def Um(b):
         def part(t, q):
-            for k in range(8):
-                op("p", lambda: P.matmul(arr("U", ub(t, q))[:, BANK * b + k:BANK * b + BANK:8], T.PKh[:], arr("R", q)[:, 15::16], False, k == 7),
-                   r=["PKh", ("R", q)], b=[("U", ub(t, q), b)])
+            u, lo, hi, key = arr("U", ub(t, q)), BANK * b, BANK * b + BANK, [("U", ub(t, q), b)]
+            if NQ * t + q not in TR:
+                for k in range(8):
+                    op("p", lambda: P.matmul(u[:, lo + k:hi:8], T.PKh[:], arr("R", q)[:, 15::16], False, k == 7), r=["PKh", ("R", q, b)], b=key)
+                return
+            for k in range(16):
+                op("p", lambda: P.matmul(u[:, lo + k:hi:16], T.IDh[:], arr("R", q)[:, lo + 15:hi:16], False, False), r=["IDh", ("R", q, b)], b=key)
+        return part
+
+    def Ur(b):
+        def part(t, q):
+            u, lo, hi, key = arr("U", ub(t, q)), BANK * b, BANK * b + BANK, [("U", ub(t, q), b)]
+            if NQ * t + q not in TR:
+                return
+            for k in range(2):
+                op("p", lambda: P.matmul(u[:, lo:hi], T.R4b[0:33, 128 * k:128 * k + 128], T.oneb[0:33, :], False, False),
+                   r=[("R4b", 0, k), ("R4b", 32, k), "oneb"], b=key)
+            op("p", lambda: P.matmul(u[:, lo:hi], T.IDh[:], arr("X", q)[:, lo:hi], False, True), r=xk(t, q, b), b=key)
         return part
 
     def Wm(b):
         def part(t, q):
-            op("v", lambda: V.tensor_tensor(arr("Wm", q)[:, b::2], arr("X", q)[:, b::2], arr("U", ub(t, q))[:, BANK * b:BANK * b + BANK], A.min),
-               r=[("X", q, 0), ("X", q, 1)], w=[("Wm", q, b)], b=[("U", ub(t, q), b)])
+            half, key = slice(BANK * b, BANK * b + BANK), [("U", ub(t, q), b)]
+            if NQ * t + q in TR:
+                op("v", lambda: V.tensor_tensor_scan(arr("S2", q)[:, half], T.mask[:, half], arr("U", ub(t, q))[:, half], 0.0, A.mult, A.max),
+                   w=[("S2", q, b)], b=key)
+            else:
+                op("v", lambda: V.tensor_tensor(arr("Wm", q)[:, b::2], arr("X", q)[:, b::2], arr("U", ub(t, q))[:, half], A.min),
+                   r=xk(t, q, b), w=[("Wm", q, b)], b=key)
         return part
 
     def Sc(t, q):
-        op("v", lambda: V.tensor_tensor_scan(arr("S2", q)[:], T.mask[:], arr("Wm", q)[:], 0.0, A.mult, A.max),
-           r=["mask", ("Wm", q, 0), ("Wm", q, 1)], w=[("S2", q, 0), ("S2", q, 1)])
+        if NQ * t + q not in TR:
+            op("v", lambda: V.tensor_tensor_scan(arr("S2", q)[:], T.mask[:, 0:CW], arr("Wm", q)[:], 0.0, A.mult, A.max),
+               r=["mask", ("Wm", q, 0), ("Wm", q, 1)], w=[("S2", q, 0), ("S2", q, 1)])
 
     def Sk(t, q):
-        op("v", lambda: V.tensor_copy(T.SL[:, cols(q)], arr("S2", q)[:, 15::16]), r=[("S2", q, 0), ("S2", q, 1)], w=[("SL", q)])
+        copy("k", t, q, T.SL[:, cols(q)], arr("S2", q)[:, 15::16], [("S2", q, 0), ("S2", q, 1)], [("SL", q)])
 
     def Cg(t, q):
-        k = VC.get(NQ * t + q, 0)
-        op("s", lambda: S.activation(arr("Y", q)[:, 16 * k:CW], T.Cx[:, 0:W].indirect(T.SL[:, cols(q, k)]), COPY),
-           r=call + [("SL", q)], w=[("Y", q, 1)] if k else [("Y", q, 0), ("Y", q, 1)])
+        k, (a, e) = VC.get(NQ * t + q, 0), CUT[t][q:q + 2]
+        op("s", lambda: S.activation(arr("Y", q)[:, 16 * k:16 * (e - a)], T.Cx[:, 0:W].indirect(T.SL[:, a + k:e]), COPY),
+           r=call + [("SL", j) for j in range(a // CH, (e - 1) // CH + 1)], w=[("Y", q, 1)] if k else [("Y", q, 0), ("Y", q, 1)])
 
     def Cv(t, q):
-        k = VC.get(NQ * t + q, 0)
+        k, a = VC.get(NQ * t + q, 0), CUT[t][q]
         if k:
-            op("v", lambda: V.tensor_copy(arr("Y", q)[:, 0:16 * k], T.Cx[:, 0:W].indirect(T.SL[:, CH * q:CH * q + k])),
-               r=call + [("SL", q)], w=[("Y", q, 0)])
+            op("v", lambda: V.tensor_copy(arr("Y", q)[:, 0:16 * k], T.Cx[:, 0:W].indirect(T.SL[:, a:a + k])),
+               r=call + [("SL", a // CH), ("SL", (a + max(k, 32) - 1) // CH)], w=[("Y", q, 0)])
 
     def Rl(t, q):
-        lst, key = (T.ou[:, 16:32], "ou") if t == 0 else (arr("NU", t)[:], ("NU", t))
+        lst, key = (T.ou[:, 16:32], "ou") if t == 0 else (arr("LI", t)[:, AU + 32:AU + 48], ("LT", t))
         op("s", lambda: S.activation(T.REL[:], T.Cx[:, 0:W].indirect(lst), COPY), r=call + [key], w=["REL"])
 
-    def pick(b, o, x, key, q):
-        rel, fd = T.REL[:, cols(q)], T.FD[:, cols(q)]
-        sums(b, [(o, T.IDh[:], x, [key]), (o, T.NIh[:], rel, ["NIh", "REL"]), (o, T.PHb[:], fd, ["PHb", ("FD", q)]), (o, T.NHb[:], fd, ["NHb"]),
-                 (o, T.IDh[:], rel, [])])
+    def pick(b, o, x, key, t, q):
+        rel, fd = T.REL[:, cut(t, q)], T.FD[:, cut(t, q)]
+        sums(b, [(o, T.IDh[:], x, [key]), (o, T.NIh[:], rel, ["NIh", "REL"]), (o, T.PHb[:], fd, ["PHb", ("FD", q)]), (o, T.NHb[:], fd, ["NHb", ("FD", q)]),
+                 (o, T.IDh[:], rel, ["REL"])])
 
     def base(t, q):
-        return (arr("BS", t)[:, cols(q)], ("BS", t, q // 2)) if t else (T.IH0[:, cols(q)], ("IH", 0, q // 2))
+        return arr("IH", t)[:, at(q, 2 * CH if t else 0)], ("IH", t, q // 2)
 
     def PTI(t, q):
-        sums(("Q", q), [(slot(q, 0), T.IDh[:], arr("IH", t)[:, cols(q)], ["IDh", ("IH", t, q // 2)])])
+        sums(("Q", q), [(slot(t, q, 0), T.IDh[:], arr("IH", t)[:, at(q)], ["IDh", ("IH", t, q // 2)])])
         x, key = base(t, q)
-        sums(("Q", q), [(slot(q, 1), T.IDh[:], x, [key]), (slot(q, 1), T.IDh[:], arr("GP", t)[:, cols(q)], [("GP", t)])])
+        sums(("Q", q), [(slot(t, q, 1), T.IDh[:], x, [key]), (slot(t, q, 1), T.IDh[:], arr("GP", t)[:, cut(t, q)], [("GP", t)])])
 
     def Cm(t, q):
-        op("v", lambda: V.tensor_tensor_scan(arr("R2", q)[:], T.mask[:], arr("Y", q)[:], 0.0, A.mult, A.max),
+        e = 16 * wid(t, q)
+        op("v", lambda: V.tensor_tensor_scan(arr("R2", q)[:, 0:e], T.mask[:, 0:e], arr("Y", q)[:, 0:e], 0.0, A.mult, A.max),
            r=["mask", ("Y", q, 0), ("Y", q, 1)], w=[("R2", q)])
 
     def Ge(t, q):
-        op("v", lambda: V.tensor_tensor(T.NEW[:, cols(q)], arr("R2", q)[:, 15::16], slot(q, 0), A.max),
+        op("v", lambda: V.tensor_tensor(T.NEW[:, cut(t, q)], arr("R2", q)[:, 15:16 * wid(t, q):16], slot(t, q, 0), A.max),
            r=[("R2", q)], w=[("NEW", q)], b=[("Q", q)])
 
     def Gb(t, q):
-        op("v", lambda: V.tensor_tensor(T.GE[:, cols(q)], T.NEW[:, cols(q)], slot(q, 1), A.is_ge),
+        op("v", lambda: V.tensor_tensor(T.GE[:, cut(t, q)], T.NEW[:, cut(t, q)], slot(t, q, 1), A.is_ge),
            r=[("NEW", q)], w=[("GE", q)], b=[("Q", q)])
 
     def Pb(t, q):
-        sums(("Q", q), [(slot(q, 2), T.BGb[:], T.GE[:, cols(q)], ["BGb", ("GE", q)])])
+        sums(("Q", q), [(slot(t, q, 2), T.BGb[:], T.GE[:, cut(t, q)], ["BGb", ("GE", q)])])
 
     def Fd(t, q):
-        op("v", lambda: V.tensor_tensor(T.FD[:, cols(q)], slot(q, 2), T.TH[:], A.is_ge), r=["TH"], w=[("FD", q)], b=[("Q", q)])
+        op("v", lambda: V.tensor_tensor(T.FD[:, cut(t, q)], slot(t, q, 2), T.TH[:, 0:wid(t, q)], A.is_ge), r=["TH"], w=[("FD", q)], b=[("Q", q)])
 
     def Pq(t, q):
-        pick(("Q", q), slot(q, 0), T.NEW[:, cols(q)], ("NEW", q), q)
+        pick(("Q", q), slot(t, q, 0), T.NEW[:, cut(t, q)], ("NEW", q), t, q)
 
     def Po(t, q):
         if t < ST - 1:
-            pick("Z", T.Z[:, cols(q)], *base(t, q), q)
+            pick("Z", T.Z[:, cols(q)], *base(t, q), t, q)
 
     def So(t, q):
         if t < ST - 1:
-            if OV:
-                op("v", lambda: V.tensor_copy(arr("OB", t)[:, two(q)], T.Z[:, two(q)]), w=[("OB", t, q)], b=["Z"])
-            else:
-                op("s", lambda: S.activation(arr("OB", t)[:, two(q)], T.Z[:, two(q)], COPY), w=[("OB", t, q)], b=["Z"])
-            send(nxt, arr("BS", t + 1)[:, two(q)], arr("OB", t)[:, two(q)], "ab%d_%d" % (t + 1, q // 2), [("OB", t, q)])
+            copy("O", t, q, arr("OL", t)[:, AT[q] + 2 * CH:AT[q] + 4 * CH], T.Z[:, CH * q:CH * q + 2 * CH], [], [("OB", t, q)], ["Z"])
 
     def Sj(t, q):
         if t == ST - 1:
-            op("v", lambda: V.tensor_copy(T.YO[:, cols(q)], slot(q, 0)), w=[("YO", q)], b=[("Q", q)])
-            send(nxt, T.YL[:, cols(q)], T.YO[:, cols(q)], "ay%d" % q, [("YO", q)])
+            copy("J", t, q, T.YO[:, cut(t, q)], slot(t, q, 0), [], [("YO", q)], [("Q", q)])
+            if q + 1 in OUTS[1:-1]:
+                a = OUTS[OUTS.index(q + 1) - 1]
+                part = slice(CH * a, CH * q + CH)
+                send(nxt, T.YL[:, part], T.YO[:, part], "ay%d" % a, [("YO", k) for k in range(a, q + 1)])
             return
-        op("v", lambda: V.tensor_copy(arr("OL", t)[:, cols(q)], slot(q, 0)), w=[("OL", t, q)], b=[("Q", q)])
-        send(nxt, arr("LI", t + 1)[:, cols(q)], arr("OL", t)[:, cols(q)], "al%d_%d" % (t + 1, q), [("OL", t, q)])
+        op("v", lambda: V.tensor_copy(arr("OL", t)[:, at(q)], slot(t, q, 0)), w=[("OL", t, q)], b=[("Q", q)])
+        part, keys = (slice(2 * CH, AT[q] + CH), [("OB", t, 0)]) if q == 2 else (at(q), [])
+        if q == 3 and MERGE:
+            return
+        send(nxt, arr("LI", t + 1)[:, part], arr("OL", t)[:, part], "al%d_%d" % (t + 1, q), [("OL", t, q)] + keys)
 
     ZU, ZL = NC, NC + 16
+
+    def ukey(t):
+        return ("IH", t, 1) if t else "u0"
 
     def Pu(t, q):
         keys = [("FD", k) for k in range(NQ)]
@@ -347,56 +440,60 @@ def rank_program(g, core, T, topo):
             op("v", lambda: V.tensor_tensor_scan(T.FL[:], T.mask[:, 0:NC], T.FD[:], 0.0, A.mult, A.max), r=keys, w=["FL"])
             return
         o = T.Z[:, ZU:ZU + 16]
-        sums("Z", [(o, T.IDh[:], arr("UU", t)[:, 0:16], [("UU", t, 0)])] + [(o, T.IDb[:], T.FD[:, a::16], ["IDb"] + keys) for a in range(16)])
+        sums("Z", [(o, T.IDh[:], arr("IH", t)[:, AU:AU + 16], [ukey(t)])] + [(o, T.IDb[:], T.FD[:, a::16], ["IDb"] + keys) for a in range(16)])
 
     def Vu(t, q):
-        uu = arr("UU", t)
         if t < ST - 1:
-            op("v", lambda: V.tensor_copy(uu[:, 16:32], T.Z[:, ZU:ZU + 16]), w=[("UU", t, 1)], b=["Z"])
-            send(nxt, arr("UU", t + 1)[:, 0:16], uu[:, 16:32], "au%d" % (t + 1), [("UU", t, 1)])
+            op("v", lambda: V.tensor_copy(arr("IH", t)[:, AU + 16:AU + 32], T.Z[:, ZU:ZU + 16]), w=[("un", t)], b=["Z"])
 
     def Pw(t, q):
-        uu, last = arr("UU", t), t == ST - 1
+        ih, last = arr("IH", t), t == ST - 1
         w = 16 if last else 32
         o = T.Z[:, ZL:ZL + w]
-        xs = [(uu[:, 0:16], [("UU", t, 0)]), (T.FL[:, 15::16], ["FL"])] if last else [(uu[:], [("UU", t, 0), ("UU", t, 1)])]
+        xs = [(ih[:, AU:AU + 16], [ukey(t)]), (T.FL[:, 15::16], ["FL"])] if last else [(ih[:, AU:AU + 32], [ukey(t), ("un", t)])]
         terms = [(o, T.IDh[:], T.K1[:, 0:w], [("K1", 0), ("K1", 1)])] + [(o, T.NIh[:], x, keys) for x, keys in xs]
         terms += [(o, T.R8b[0:1, 0:128], T.oneb[0:1, 0:w], ["R8p", "oneb"]), (o, T.R8b[0:1, 128:256], T.oneb[0:1, 0:w], ["R8n"])]
         terms += [(o, T.IDh[:], x, []) for x, keys in xs]
         if not last:
             o1 = T.Z[:, ZL:ZL + 16]
-            terms += [(o1, T.PKh[:], uu[:, 0:16], []), (o1, T.NKh[:], uu[:, 16:32], []), (o, T.IDh[:], T.K2[:], [("K2", 0), ("K2", 1)])]
+            terms += [(o1, T.PKh[:], ih[:, AU:AU + 16], []), (o1, T.NKh[:], ih[:, AU + 16:AU + 32], []),
+                      (o, T.IDh[:], T.K2[:], [("K2", 0), ("K2", 1)])]
         sums("Z", terms)
 
     def Vy(t, q):
         if t == ST - 1:
-            op("v", lambda: V.tensor_copy(T.YC[:], T.Z[:, ZL:ZL + 16]), w=["YC"], b=["Z"])
-            send(nxt, T.YCL[:], T.YC[:], "ayc", ["YC"])
-            return
-        op("v", lambda: V.tensor_copy(arr("RU", t)[:], T.Z[:, ZL:ZL + 32]), w=[("RU", t)], b=["Z"])
-        send(nxt, arr("NU", t + 1)[:], arr("RU", t)[:, 16:32], "an%d" % (t + 1), [("RU", t)])
+            op("v", lambda: V.tensor_copy(T.YO[:, NC:NC + 16], T.Z[:, ZL:ZL + 16]), w=["YC"], b=["Z"])
+        else:
+            op("v", lambda: V.tensor_copy(arr("OL", t)[:, AU:AU + 48], T.Z[:, ZU:ZU + 48]), w=[("RU", t)], b=["Z"])
+
+    def Tail(t, q):
+        if t == ST - 1:
+            a = OUTS[-2]
+            send(nxt, T.YL[:, CH * a:NC + 16], T.YO[:, CH * a:NC + 16], "ay%d" % a, [("YO", k) for k in range(a, NQ)] + ["YC"])
+        else:
+            a = AT[NQ - 1] + (0 if MERGE else CH)
+            send(nxt, arr("LI", t + 1)[:, a:AU + 48], arr("OL", t)[:, a:AU + 48], "at%d" % (t + 1),
+                 [("OB", t, 2), ("RU", t)] + [("OL", t, 3)] * MERGE)
 
     def Scat(t, q):
         if t < ST - 1:
-            op("v", lambda: V.tensor_copy(T.Cx[:].indirect(arr("RU", t)[:, 0:16]), T.NEW[:]),
+            op("v", lambda: V.tensor_copy(T.Cx[:].indirect(arr("OL", t)[:, AU + 16:AU + 32]), T.NEW[:]),
                r=[("RU", t)] + [("NEW", k) for k in range(NQ)], w=call)
 
-    parts = {"I": Ig, "i": Ih, "A": Gp, "L": Lg, "l": Lv, "M": Mx, "X": Ux, "U": Um(0), "V": Um(1), "W": Wm(0), "Z": Wm(1),
+    parts = {"I": Ig, "i": Ih, "A": Gp, "L": Lg, "K": Lh, "l": Lv, "M": Mx(0), "N": Mx(1), "X": Ux(0), "Y": Ux(1), "U": Um(0), "V": Um(1), "E": Ur(0), "F": Ur(1), "W": Wm(0), "Z": Wm(1),
              "S": Sc, "k": Sk, "C": Cg, "c": Cv, "R": Rl, "P": PTI,
-             "m": Cm, "G": Ge, "g": Gb, "B": Pb, "f": Fd, "Q": Pq, "J": Sj, "o": Po, "O": So, "u": Pu, "v": Vu, "w": Pw, "y": Vy, "x": Scat}
-    for t, order in [(0, START)] + [(t, STEP) for t in range(ST - 1)] + [(ST - 1, LAST)]:
+             "m": Cm, "G": Ge, "g": Gb, "B": Pb, "f": Fd, "Q": Pq, "J": Sj, "o": Po, "O": So, "u": Pu, "v": Vu, "w": Pw, "y": Vy, "z": Tail, "x": Scat}
+    for t, order in [(0, ORDER)]:
         for tok in order.split():
-            n = NQ * t + int(tok[1:])
-            if n < NN:
-                parts[tok[0]](n // NQ, n % NQ)
+            parts[tok[0]](*divmod(int(tok[1:]), NQ))
 
-    for q in range(NQ):
-        wait("y", "ay%d" % q, len(topo.engines(prv, core)))
-        g.sync.dma_start(T.yi[:, cols(q)], T.YL[:, cols(q)]).then_inc(T.sem.dout, 16)
-    wait("s", "ayc", len(topo.engines(prv, core)))
-    S.dma_start(T.yc[:], T.YCL[:]).then_inc(T.sem.dyc, 16)
+    for a, e in zip(OUTS, OUTS[1:]):
+        wait("y", "ay%d" % a, len(topo.engines(prv, core)))
+        g.sync.dma_start(T.yi[:, CH * a:CH * e], T.YL[:, CH * a:CH * e]).then_inc(T.sem.dout, 16)
+    wait("s", "ay%d" % OUTS[-2], len(topo.engines(prv, core)))
+    S.dma_start(T.yc[:], T.YL[:, NC:NC + 16]).then_inc(T.sem.dyc, 16)
     wait("s", "dyc", 16)
-    wait("y", "dout", 16 * NQ)
+    wait("y", "dout", 16 * (len(OUTS) - 1))
     for q in own:
         wait("g", own[q], cnt[q])
     wait("g", "loc", tot["loc"])

from concourse.bass import DstId, RemoteDMATransfer
from concourse.mybir import dt, AluOpType, ActivationFunctionType

NQ, CH, ST, W = 4, 64, 3, 2048
CW = CH * 16
NC = NQ * CH
NN = NQ * ST
BANK = 512
NUB = 2
NQB = 7 - 2 * NUB
CM = 64
AT, AU = [0, CH, 4 * CH, 5 * CH], 8 * CH
GAPAT = 4
MERGE = 0
OUTS = [0, 1, 2, 3, 4]
LCUT = [0, 64, 128, 192, 256]
CUT = [[0, 64, 128, 192, 256]] * (ST - 1) + [LCUT]
TR = {10}
WHO = dict({k: "g" for k in "A0 k4 k5 k6 k8 k9 k10 i0 i2 i4 i6 i8 i10".split()}, **{k: "s" for k in "J8 J9".split()})
HUGE = 2.0 ** 40
ULP8 = 1.5 * 2.0 ** 26
VL = {0: 32, 1: 16, 4: 8, 5: 16, 8: 8, 9: 16}
VC = {3: 16, 7: 16, 11: 24}
ORDER = """
I0 L0 l0 I1 L1 X0 Y0 M0 V0 U0 l1 I2 Z0 W0 M1 i0 S0 I3 A0 k0 X1 Y1 V1 U1 L2 L3 C0 Z1 W1 M2 S1 M3 X2 Y2 U2 P1 V2 Y3 X3 U3 P0 V3 k1 W2
Z2 m0 S2 i2 G0 W3 k2 g0 Z3 R0 C1 C2 B0 f0 Q0 m1 J0 S3 G1 k3 g1 C3 m2 P3 B1 P2 f1 Q1 o1 G2 c3 g2 B2 o0 J1 m3 f2 L4 L5 O0 G3 Q2 l4 g3
J2 o2 X4 B3 Y4 M4 f3 l5 U4 V4 Q3 W4 J3 Z4 u0 v0 Y5 w0 o3 M5 S4 V5 X5 U5 y0 O2 L6 z0 k4 x0 i4 L7 C4 Z5 W5 M6 S5 M7 X6 Y6 U6 P5 V6 Y7
X7 U7 P4 V7 k5 W6 Z6 m4 S6 i6 G4 W7 k6 g4 Z7 R4 C5 C6 B4 f4 Q4 m5 J4 S7 G5 k7 g5 C7 m6 P7 B5 P6 f5 Q5 o5 G6 c7 g6 B6 o4 J5 m7 f6 L8
L9 O4 G7 Q6 l8 g7 J6 o6 X8 B7 Y8 M8 f7 l9 U8 V8 Q7 W8 J7 Z8 u4 v4 Y9 w4 o7 M9 S8 V9 X9 U9 y4 O6 L10 K10 z4 k8 x4 i8 L11 C8 Y10 X10
M10 Z9 U10 E10 W9 N10 S9 M11 W10 m8 V10 F10 X11 U11 P8 Y11 V11 R8 k9 Z10 G8 C9 W11 g8 Z11 m9 P9 B8 S11 G9 k11 g9 k10 C10 f8 i10 c11
C11 P10 Q8 B9 P11 m10 J8 f9 Q9 m11 G10 G11 J9 g10 B10 g11 f10 B11 f11 u8 Q10 Q11 J10 w8 J11 y8 z8
"""

SCRATCH = {
    "Lt": ("sbuf", [128, W], "int32"),
    "Cx": ("sbuf", [128, 2 * W], "int32"),
    "gapi": ("sbuf", [128, NC], "int32"),
    "cui": ("sbuf", [128, 16], "int32"),
    "ones": ("sbuf", [128, 128], "float32"),
    "tI": ("sbuf", [128, 128], "float32"),
    "tB": ("sbuf", [128, 128], "float32"),
    "tC": ("sbuf", [128, 128], "float32"),
    "mask": ("sbuf", [128, 16 * CM], "float16"),
    "IDh": ("sbuf", [128, 128], "float16"),
    "NIh": ("sbuf", [128, 128], "float16"),
    "NKh": ("sbuf", [128, 128], "float16"),
    "PKh": ("sbuf", [128, 128], "float16"),
    "IDb": ("sbuf", [128, 128], "bfloat16"),
    "BGb": ("sbuf", [128, 128], "bfloat16"),
    "PHb": ("sbuf", [128, 128], "bfloat16"),
    "NHb": ("sbuf", [128, 128], "bfloat16"),
    "R8b": ("sbuf", [128, 256], "bfloat16"),
    "R4b": ("sbuf", [128, 256], "bfloat16"),
    "drop": ("sbuf", [128, BANK], "float16"),
    "oneb": ("sbuf", [128, BANK], "bfloat16"),
    "K1": ("sbuf", [128, 32], "float16"),
    "K2": ("sbuf", [128, 32], "float16"),
    "TH": ("sbuf", [128, CM], "float32"),
    "tj": ("sbuf", [128, CM], "int32"),
    "tk": ("sbuf", [128, CM], "int32"),
    "j8": ("sbuf", [128, 16], "int32"),
    "jq": ("sbuf", [128, 32], "int32"),
    "j8a": ("sbuf", [128, 16], "int32"),
    "i8": ("sbuf", [128, 32], "int32"),
    "ca": ("sbuf", [128, 16], "int32"),
    "cb": ("sbuf", [128, 16], "int32"),
    "cc": ("sbuf", [128, 32], "int32"),
    "ou": ("sbuf", [128, 32], "uint16"),
    "SL": ("sbuf", [128, NC], "uint16"),
    "NEW": ("sbuf", [128, NC], "float16"),
    "GE": ("sbuf", [128, NC], "bfloat16"),
    "FL": ("sbuf", [128, NC], "float16"),
    "REL": ("sbuf", [128, NC], "float16"),
    "YO": ("sbuf", [128, NC + 16], "float32"),
    "YL": ("sbuf", [128, NC + 16], "float32"),
    "FD": ("sbuf", [128, NC], "bfloat16"),
    "Z": ("psum", [128, BANK], "float32"),
}
for _q in range(NUB):
    SCRATCH["U%d" % _q] = ("psum", [128, 2 * BANK], "float32")
for _q in range(NQB):
    SCRATCH["Q%d" % _q] = ("psum", [128, BANK], "float32")
for _q in range(NQ):
    for _n in ("X", "R", "Wm", "S2", "Y", "R2"):
        SCRATCH["%s%d" % (_n, _q)] = ("sbuf", [128, 16 * CM if _n in ("Y", "R2") else CW], "float16")
for _t in range(ST):
    SCRATCH["LI%d" % _t] = ("sbuf", [128, AU + 48], "uint16")
    SCRATCH["IH%d" % _t] = ("sbuf", [128, AU + 32], "float16")
    SCRATCH["GP%d" % _t] = ("sbuf", [128, NC], "float16")
    if _t < ST - 1:
        SCRATCH["OL%d" % _t] = ("sbuf", [128, AU + 48], "uint16")

SEMAPHORES = ["sv", "ss", "sp", "sg", "dla", "dcu", "dgp", "loc", "dout", "dyc"]
for _t in range(1, ST):
    SEMAPHORES += ["at%d" % _t, "ag%d" % _t] + ["al%d_%d" % (_t, _q) for _q in range(NQ)]
SEMAPHORES += ["ay%d" % _q for _q in range(NQ)] + ["dck%d" % _q for _q in range(NQ)]


def rank_program(g, core, T, topo):
    rank = T.rank_of(core)
    if rank is None:
        return
    A, COPY = AluOpType, ActivationFunctionType.Copy
    cores = list(T.cores)
    nr = len(cores)
    ahead = {k: cores[(rank + k) % nr] for k in range(1 - ST, ST)}
    nxt, prv = ahead[1], ahead[-1]
    V, S, P = g.vector, g.scalar, g.tensor
    que = {"v": V, "s": S, "p": P, "g": g, "y": g.sync}
    own = {"v": "sv", "s": "ss", "p": "sp", "g": "sg"}
    cnt = {"v": 0, "s": 0, "p": 0, "g": 0}
    known, seen, wr, rd, bank, tot = {q: {} for q in que}, {}, {}, {}, {}, {"loc": 0}

    def wait(q, sem, val):
        if known[q].get(sem, 0) < val:
            que[q].wait_ge(T.sem[sem], val)
            for s, v in list(seen.get((sem, val), {}).items()) + [(sem, val)]:
                known[q][s] = max(known[q].get(s, 0), v)

    def deps(q, r, w, b=()):
        need, mine = {}, own.get(q)
        toks = [wr[k] for k in list(r) + list(w) if k in wr]
        toks += [(s, v) for k in w for s, v in rd.get(k, {}).items() if s != mine]
        toks += [bank[k] for k in b if k in bank and bank[k][0] != mine]
        for sem, val in toks:
            need[sem] = max(need.get(sem, 0), val)
        for sem, val in sorted(need.items(), key=lambda x: -sum(seen.get(x, {}).get(s, 0) >= v for s, v in need.items())):
            wait(q, sem, val)

    def op(q, fn, r=(), w=(), b=()):
        b = [("Q", k[1] % NQB) if k[0] == "Q" else k for k in b]
        deps(q, r, w, b)
        fn().then_inc(T.sem[own[q]], 1)
        cnt[q] += 1
        seen[(own[q], cnt[q])] = dict(known[q])
        for k in r:
            rd.setdefault(k, {})[own[q]] = cnt[q]
        for k in w:
            wr[k] = (own[q], cnt[q])
            rd[k] = {}
        for k in b:
            bank[k] = (own[q], cnt[q])

    def sums(b, terms):
        for i, (o, l, x, r) in enumerate(terms):
            op("p", lambda: P.matmul(o, l, x, i == 0, i == len(terms) - 1), r=r, b=[b])

    def copy(part, t, q, out, in_, r, w, b=()):
        who = WHO.get("%s%d" % (part, NQ * t + q), "v")
        call = {"v": lambda: V.tensor_copy(out, in_), "s": lambda: S.activation(out, in_, COPY),
                "g": lambda: g.affine_select(out, in_, [[0, out.shape[1]]], A.is_ge, 0.0, 0, 0)}
        op(who, call[who], r, w, b)

    def load(q, out, in_, sem, key):
        que[q].dma_start(out, in_).then_inc(T.sem[sem], 16)
        wr[key] = (sem, 16)

    def send(dst, out, in_, sem, r):
        deps("g", r, ())
        rid, pid, _ = topo.addr(dst)
        g.remote_dma(out, in_, T.sem[sem], T.sem.loc, pid, rid, topo.mask(core, dst))
        tot["loc"] += len(topo.engines(core, dst))

    def apart(r):
        src = cores[r % nr]
        near, far = topo.engines(src, cores[(r + 1) % nr]), topo.engines(src, cores[(r + 2) % nr])
        rest = [e for e in near if e not in far]
        return (rest, far) if rest else (near[:len(near) // 2], far[len(far) // 2:])

    def send2(out1, out2, in_, sem1, sem2, r):
        deps("g", r, ())
        moves = []
        for k, out, sem, eng in zip((1, 2), (out1, out2), (sem1, sem2), apart(rank)):
            rid, pid, _ = topo.addr(ahead[k])
            moves.append(RemoteDMATransfer(dst_ids=[DstId(rid=rid, pnc=pid)], dma_engine_mask=sum(1 << e for e in eng),
                                           remote_sem=T.sem[sem], src=in_, dst=out))
            tot["loc"] += len(eng)
        g.remote_dma_fused(moves, local_sem=T.sem.loc)

    def lands(src, sem, key, count=None):
        wr[key] = (sem, count or len(topo.engines(src, core)))

    def arr(name, k):
        return T["%s%d" % (name, k)]

    CB = W // NQ
    call = [("C", q) for q in range(NQ)]
    load("s", T.cui[:], T.cu[:], "dcu", "cui")
    load("y", T.Cx[:, 0:CB], T.ck[:, 0:CB], "dck0", ("C", 0))
    load("y", T.Lt[:], T.la[:], "dla", "Lt")
    for q in range(1, NQ + 1):
        if q == GAPAT:
            load("y", T.gapi[:], T.gap[:], "dgp", "gapi")
        if q < NQ:
            load("y", T.Cx[:, CB * q:CB * q + CB], T.ck[:, CB * q:CB * q + CB], "dck%d" % q, ("C", q))
    for t in (1, 2):
        lands(prv, "at%d" % t, ("LT", t))
        for q in range(NQ):
            lands(prv, "al%d_%d" % (t, q), ("LI", t, q))
        lands(ahead[-t], "ag%d" % t, ("GP", t), len(apart(rank - t)[t - 1]))

    def scaled(name, src, k):
        if name in ("IDb", "NIh", "PHb"):
            op("s", lambda: S.activation(T[name][:], T[src][:], COPY, scale=k), r=[src], w=[name])
        else:
            op("v", lambda: V.tensor_scalar(T[name][:], T[src][:], k, None, A.mult), r=[src], w=[name])

    op("v", lambda: V.memset(T.ones[:], 1.0), w=["ones"])
    op("g", lambda: g.iota(T.j8[:], [[0, 16]], 0, 8), w=["j8"])
    op("g", lambda: g.iota(T.jq[:, 0:16], [[0, 4], [128, 4]], 0, 0), w=[("jq", 0)])
    op("g", lambda: g.iota(T.jq[:, 16:32], [[128, 16]], 0, 0), w=[("jq", 1)])
    op("g", lambda: g.iota(T.tj[:], [[-1, CM]], 128, 1), w=["tj"])
    op("g", lambda: g.affine_select(T.tI[:], T.ones[:], [[-1, 128]], A.is_equal, 0.0, 0, 1), r=["ones"], w=["tI"])
    op("g", lambda: g.affine_select(T.tC[:], T.ones[:], [[-16, 8], [0, 16]], A.is_ge, 0.0, 0, 1), r=["ones"], w=["tC"])
    op("g", lambda: g.affine_select(T.tB[:], T.tC[:], [[16, 8], [0, 16]], A.is_ge, 0.0, 15, -1), r=["tC"], w=["tB"])
    op("v", lambda: V.memset(T.mask[:], 1.0), w=["mask"])
    op("v", lambda: V.memset(T.oneb[:], 1.0), w=["oneb"])
    op("v", lambda: V.memset(T.mask[:, 0::16], 0.0), w=["mask"])
    op("v", lambda: V.tensor_scalar(T.j8a[:], T.j8[:], 127, None, A.bitwise_and), r=["j8"], w=["j8a"])
    op("v", lambda: V.memset(T.R8b[0:1, 0:128], ULP8), w=["R8p"])
    op("v", lambda: V.memset(T.R8b[0:1, 128:256], -ULP8), w=["R8n"])
    for k in range(2):
        op("v", lambda: V.tensor_tensor(T.i8[:, 16 * k:16 * k + 16], T.j8a[:], T.jq[:, 16 * k:16 * k + 16], A.add), r=["j8a", ("jq", k)], w=[("i8", k)])
    op("v", lambda: V.tensor_scalar(T.ca[:], T.cui[:], 1, None, A.add), r=["cui"], w=["ca"])
    op("v", lambda: V.tensor_tensor(T.cc[:, 0:16], T.cui[:], T.i8[:, 0:16], A.add), r=["cui", ("i8", 0)], w=[("cc", 0)])
    op("v", lambda: V.tensor_scalar(T.cb[:], T.ca[:], 7, None, A.bitwise_and), r=["ca"], w=["cb"])
    op("v", lambda: V.tensor_copy(T.IH0[:, AU:AU + 16], T.cui[:]), r=["cui"], w=["u0"])
    op("v", lambda: V.tensor_tensor(T.cc[:, 16:32], T.cb[:], T.i8[:, 16:32], A.add), r=["cb", ("i8", 1)], w=[("cc", 1)])
    scaled("NKh", "tI", -float(W))
    op("v", lambda: V.tensor_copy(T.ou[:], T.cc[:]), r=[("cc", 0), ("cc", 1)], w=["ou"])
    for name, src, k in (("PKh", "tI", float(W)), ("IDh", "tI", 1.0), ("NIh", "tI", -1.0), ("IDb", "tI", 1.0),
                         ("BGb", "tB", 1.0), ("PHb", "tB", HUGE), ("NHb", "tB", -HUGE)):
        scaled(name, src, k)
    op("s", lambda: S.activation(T.drop[:], T.mask[:, 1:BANK + 1], COPY, bias=-float(W), scale=float(W)), r=["mask"], w=["drop"])
    op("v", lambda: V.memset(T.R4b[0:64, :], 0.0), w=["R4b"])
    for row, val in ((0, 4096.0), (32, 1.5 * 2.0 ** 35)):
        for k in range(2):
            op("v", lambda: V.memset(T.R4b[row:row + 1, 128 * k:128 * k + 128], (1 - 2 * k) * val), r=["R4b"], w=[("R4b", row, k)])
    op("v", lambda: V.tensor_scalar(T.tk[:], T.tj[:], 15, None, A.bitwise_and), r=["tj"], w=["tk"])
    op("v", lambda: V.memset(T.K1[:, 0:16], 3.5), w=[("K1", 0)])
    op("v", lambda: V.memset(T.K1[:, 16:32], 2.5), w=[("K1", 1)])
    op("v", lambda: V.tensor_scalar(T.TH[:], T.tk[:], 1024.0, 2.5, A.mult, A.add), r=["tk"], w=["TH"])
    op("v", lambda: V.tensor_scalar(T.K2[:, 0:16], T.i8[:, 16:32], float(W), None, A.add), r=[("i8", 1)], w=[("K2", 0)])
    op("v", lambda: V.tensor_scalar(T.K2[:, 16:32], T.i8[:, 16:32], 1.0, None, A.add), r=[("i8", 1)], w=[("K2", 1)])

    def cols(q, a=0):
        return slice(CH * q + a, CH * q + CH)

    def at(q, a=0):
        return slice(AT[q] + a, AT[q] + a + CH)

    def lk(t, q):
        return ("LT", t) if MERGE and t and q == NQ - 1 else ("LI", t, q)

    def cut(t, q):
        return slice(CUT[t][q], CUT[t][q + 1])

    def wid(t, q):
        return CUT[t][q + 1] - CUT[t][q]

    def slot(t, q, k):
        a = 3 * CM * (q // NQB) + wid(t, q) * k
        return arr("Q", q % NQB)[:, a:a + wid(t, q)]

    def ub(t, q):
        return (NQ * t + q) % NUB

    def Ig(t, q):
        op("v", lambda: V.tensor_copy(T.LI0[:, at(q)], T.Cx[:, CB * q:CB * q + CB].indirect(T.ou[:, 4 * q:4 * q + 4])),
           r=[("C", q), "ou"], w=[("LI", 0, q)])

    def Ih(t, q):
        part = slice(AT[q], AT[q] + 2 * CH if t == 0 else AU + 16 if q else AT[2])
        keys = [lk(t, q), lk(t, q + 1)] + ([] if t == 0 else [("LT", t)] if q else [("LI", t, 2)])
        copy("i", t, q, arr("IH", t)[:, part], arr("LI", t)[:, part], keys, [("IH", t, q // 2)])

    def Gp(t, q):
        copy("A", t, q, T.GP0[:], T.gapi[:], ["gapi"], [("GP", 0)])
        send2(T.GP1[:], T.GP2[:], T.GP0[:], "ag1", "ag2", [("GP", 0)])

    def Lg(t, q):
        k, e = VL.get(NQ * t + q, 0), CH // 2 if NQ * t + q in TR else CH
        if k < e:
            op("s", lambda: S.activation(arr("X", q)[:, 16 * k:16 * e], T.Lt[:, 0:W].indirect(arr("LI", t)[:, AT[q] + k:AT[q] + e]), COPY),
               r=["Lt", lk(t, q)], w=[("X", q, j) for j in range(1 if k else 0, 2 if e < CH else 3)])

    def Lh(t, q):
        if NQ * t + q in TR:
            op("s", lambda: S.activation(arr("X", q)[:, BANK:CW], T.Lt[:, 0:W].indirect(arr("LI", t)[:, AT[q] + CH // 2:AT[q] + CH]), COPY),
               r=["Lt", lk(t, q)], w=[("X", q, 2)])

    def Lv(t, q):
        k = VL.get(NQ * t + q, 0)
        if k:
            op("v", lambda: V.tensor_copy(arr("X", q)[:, 0:16 * k], T.Lt[:, 0:W].indirect(arr("LI", t)[:, AT[q]:AT[q] + k])),
               r=["Lt", lk(t, q)], w=[("X", q, 0)])

    def xk(t, q, b):
        return [("X", q, j) for j in (((0, 1), (2,))[b] if NQ * t + q in TR else (0, 1, 2))]

    def Mx(b):
        def part(t, q):
            half = slice(BANK * b, BANK * b + BANK)
            if NQ * t + q in TR:
                op("v", lambda: V.tensor_tensor_scan(arr("R", q)[:, half], arr("X", q)[:, half], T.drop[:], 0.0, A.max, A.add),
                   r=["drop"] + xk(t, q, b), w=[("R", q, b)])
            elif b == 0:
                op("v", lambda: V.tensor_tensor_scan(arr("R", q)[:], T.mask[:, 0:CW], arr("X", q)[:], 0.0, A.mult, A.max),
                   r=["mask"] + xk(t, q, b), w=[("R", q, 0), ("R", q, 1)])
        return part

    def Ux(b):
        def part(t, q):
            half = slice(BANK * b, BANK * b + BANK)
            m, x = ("NIh", arr("X", q)[:, half]) if NQ * t + q in TR else ("NKh", arr("X", q)[:, b::2])
            op("p", lambda: P.matmul(arr("U", ub(t, q))[:, half], T[m][:], x, True, False), r=[m] + xk(t, q, b), b=[("U", ub(t, q), b)])
        return part

    def Um(b):
        def part(t, q):
            u, lo, hi, key = arr("U", ub(t, q)), BANK * b, BANK * b + BANK, [("U", ub(t, q), b)]
            if NQ * t + q not in TR:
                for k in range(8):
                    op("p", lambda: P.matmul(u[:, lo + k:hi:8], T.PKh[:], arr("R", q)[:, 15::16], False, k == 7), r=["PKh", ("R", q, b)], b=key)
                return
            for k in range(16):
                op("p", lambda: P.matmul(u[:, lo + k:hi:16], T.IDh[:], arr("R", q)[:, lo + 15:hi:16], False, False), r=["IDh", ("R", q, b)], b=key)
        return part

    def Ur(b):
        def part(t, q):
            u, lo, hi, key = arr("U", ub(t, q)), BANK * b, BANK * b + BANK, [("U", ub(t, q), b)]
            if NQ * t + q not in TR:
                return
            for k in range(2):
                op("p", lambda: P.matmul(u[:, lo:hi], T.R4b[0:33, 128 * k:128 * k + 128], T.oneb[0:33, :], False, False),
                   r=[("R4b", 0, k), ("R4b", 32, k), "oneb"], b=key)
            op("p", lambda: P.matmul(u[:, lo:hi], T.IDh[:], arr("X", q)[:, lo:hi], False, True), r=xk(t, q, b), b=key)
        return part

    def Wm(b):
        def part(t, q):
            half, key = slice(BANK * b, BANK * b + BANK), [("U", ub(t, q), b)]
            if NQ * t + q in TR:
                op("v", lambda: V.tensor_tensor_scan(arr("S2", q)[:, half], T.mask[:, half], arr("U", ub(t, q))[:, half], 0.0, A.mult, A.max),
                   w=[("S2", q, b)], b=key)
            else:
                op("v", lambda: V.tensor_tensor(arr("Wm", q)[:, b::2], arr("X", q)[:, b::2], arr("U", ub(t, q))[:, half], A.min),
                   r=xk(t, q, b), w=[("Wm", q, b)], b=key)
        return part

    def Sc(t, q):
        if NQ * t + q not in TR:
            op("v", lambda: V.tensor_tensor_scan(arr("S2", q)[:], T.mask[:, 0:CW], arr("Wm", q)[:], 0.0, A.mult, A.max),
               r=["mask", ("Wm", q, 0), ("Wm", q, 1)], w=[("S2", q, 0), ("S2", q, 1)])

    def Sk(t, q):
        copy("k", t, q, T.SL[:, cols(q)], arr("S2", q)[:, 15::16], [("S2", q, 0), ("S2", q, 1)], [("SL", q)])

    def Cg(t, q):
        k, (a, e) = VC.get(NQ * t + q, 0), CUT[t][q:q + 2]
        op("s", lambda: S.activation(arr("Y", q)[:, 16 * k:16 * (e - a)], T.Cx[:, 0:W].indirect(T.SL[:, a + k:e]), COPY),
           r=call + [("SL", j) for j in range(a // CH, (e - 1) // CH + 1)], w=[("Y", q, 1)] if k else [("Y", q, 0), ("Y", q, 1)])

    def Cv(t, q):
        k, a = VC.get(NQ * t + q, 0), CUT[t][q]
        if k:
            op("v", lambda: V.tensor_copy(arr("Y", q)[:, 0:16 * k], T.Cx[:, 0:W].indirect(T.SL[:, a:a + k])),
               r=call + [("SL", a // CH), ("SL", (a + max(k, 32) - 1) // CH)], w=[("Y", q, 0)])

    def Rl(t, q):
        lst, key = (T.ou[:, 16:32], "ou") if t == 0 else (arr("LI", t)[:, AU + 32:AU + 48], ("LT", t))
        op("s", lambda: S.activation(T.REL[:], T.Cx[:, 0:W].indirect(lst), COPY), r=call + [key], w=["REL"])

    def pick(b, o, x, key, t, q):
        rel, fd = T.REL[:, cut(t, q)], T.FD[:, cut(t, q)]
        sums(b, [(o, T.IDh[:], x, [key]), (o, T.NIh[:], rel, ["NIh", "REL"]), (o, T.PHb[:], fd, ["PHb", ("FD", q)]), (o, T.NHb[:], fd, ["NHb", ("FD", q)]),
                 (o, T.IDh[:], rel, ["REL"])])

    def base(t, q):
        return arr("IH", t)[:, at(q, 2 * CH if t else 0)], ("IH", t, q // 2)

    def PTI(t, q):
        sums(("Q", q), [(slot(t, q, 0), T.IDh[:], arr("IH", t)[:, at(q)], ["IDh", ("IH", t, q // 2)])])
        x, key = base(t, q)
        sums(("Q", q), [(slot(t, q, 1), T.IDh[:], x, [key]), (slot(t, q, 1), T.IDh[:], arr("GP", t)[:, cut(t, q)], [("GP", t)])])

    def Cm(t, q):
        e = 16 * wid(t, q)
        op("v", lambda: V.tensor_tensor_scan(arr("R2", q)[:, 0:e], T.mask[:, 0:e], arr("Y", q)[:, 0:e], 0.0, A.mult, A.max),
           r=["mask", ("Y", q, 0), ("Y", q, 1)], w=[("R2", q)])

    def Ge(t, q):
        op("v", lambda: V.tensor_tensor(T.NEW[:, cut(t, q)], arr("R2", q)[:, 15:16 * wid(t, q):16], slot(t, q, 0), A.max),
           r=[("R2", q)], w=[("NEW", q)], b=[("Q", q)])

    def Gb(t, q):
        op("v", lambda: V.tensor_tensor(T.GE[:, cut(t, q)], T.NEW[:, cut(t, q)], slot(t, q, 1), A.is_ge),
           r=[("NEW", q)], w=[("GE", q)], b=[("Q", q)])

    def Pb(t, q):
        sums(("Q", q), [(slot(t, q, 2), T.BGb[:], T.GE[:, cut(t, q)], ["BGb", ("GE", q)])])

    def Fd(t, q):
        op("v", lambda: V.tensor_tensor(T.FD[:, cut(t, q)], slot(t, q, 2), T.TH[:, 0:wid(t, q)], A.is_ge), r=["TH"], w=[("FD", q)], b=[("Q", q)])

    def Pq(t, q):
        pick(("Q", q), slot(t, q, 0), T.NEW[:, cut(t, q)], ("NEW", q), t, q)

    def Po(t, q):
        if t < ST - 1:
            pick("Z", T.Z[:, cols(q)], *base(t, q), t, q)

    def So(t, q):
        if t < ST - 1:
            copy("O", t, q, arr("OL", t)[:, AT[q] + 2 * CH:AT[q] + 4 * CH], T.Z[:, CH * q:CH * q + 2 * CH], [], [("OB", t, q)], ["Z"])

    def Sj(t, q):
        if t == ST - 1:
            copy("J", t, q, T.YO[:, cut(t, q)], slot(t, q, 0), [], [("YO", q)], [("Q", q)])
            if q + 1 in OUTS[1:-1]:
                a = OUTS[OUTS.index(q + 1) - 1]
                part = slice(CH * a, CH * q + CH)
                send(nxt, T.YL[:, part], T.YO[:, part], "ay%d" % a, [("YO", k) for k in range(a, q + 1)])
            return
        op("v", lambda: V.tensor_copy(arr("OL", t)[:, at(q)], slot(t, q, 0)), w=[("OL", t, q)], b=[("Q", q)])
        part, keys = (slice(2 * CH, AT[q] + CH), [("OB", t, 0)]) if q == 2 else (at(q), [])
        if q == 3 and MERGE:
            return
        send(nxt, arr("LI", t + 1)[:, part], arr("OL", t)[:, part], "al%d_%d" % (t + 1, q), [("OL", t, q)] + keys)

    ZU, ZL = NC, NC + 16

    def ukey(t):
        return ("IH", t, 1) if t else "u0"

    def Pu(t, q):
        keys = [("FD", k) for k in range(NQ)]
        if t == ST - 1:
            op("v", lambda: V.tensor_tensor_scan(T.FL[:], T.mask[:, 0:NC], T.FD[:], 0.0, A.mult, A.max), r=keys, w=["FL"])
            return
        o = T.Z[:, ZU:ZU + 16]
        sums("Z", [(o, T.IDh[:], arr("IH", t)[:, AU:AU + 16], [ukey(t)])] + [(o, T.IDb[:], T.FD[:, a::16], ["IDb"] + keys) for a in range(16)])

    def Vu(t, q):
        if t < ST - 1:
            op("v", lambda: V.tensor_copy(arr("IH", t)[:, AU + 16:AU + 32], T.Z[:, ZU:ZU + 16]), w=[("un", t)], b=["Z"])

    def Pw(t, q):
        ih, last = arr("IH", t), t == ST - 1
        w = 16 if last else 32
        o = T.Z[:, ZL:ZL + w]
        xs = [(ih[:, AU:AU + 16], [ukey(t)]), (T.FL[:, 15::16], ["FL"])] if last else [(ih[:, AU:AU + 32], [ukey(t), ("un", t)])]
        terms = [(o, T.IDh[:], T.K1[:, 0:w], [("K1", 0), ("K1", 1)])] + [(o, T.NIh[:], x, keys) for x, keys in xs]
        terms += [(o, T.R8b[0:1, 0:128], T.oneb[0:1, 0:w], ["R8p", "oneb"]), (o, T.R8b[0:1, 128:256], T.oneb[0:1, 0:w], ["R8n"])]
        terms += [(o, T.IDh[:], x, []) for x, keys in xs]
        if not last:
            o1 = T.Z[:, ZL:ZL + 16]
            terms += [(o1, T.PKh[:], ih[:, AU:AU + 16], []), (o1, T.NKh[:], ih[:, AU + 16:AU + 32], []),
                      (o, T.IDh[:], T.K2[:], [("K2", 0), ("K2", 1)])]
        sums("Z", terms)

    def Vy(t, q):
        if t == ST - 1:
            op("v", lambda: V.tensor_copy(T.YO[:, NC:NC + 16], T.Z[:, ZL:ZL + 16]), w=["YC"], b=["Z"])
        else:
            op("v", lambda: V.tensor_copy(arr("OL", t)[:, AU:AU + 48], T.Z[:, ZU:ZU + 48]), w=[("RU", t)], b=["Z"])

    def Tail(t, q):
        if t == ST - 1:
            a = OUTS[-2]
            send(nxt, T.YL[:, CH * a:NC + 16], T.YO[:, CH * a:NC + 16], "ay%d" % a, [("YO", k) for k in range(a, NQ)] + ["YC"])
        else:
            a = AT[NQ - 1] + (0 if MERGE else CH)
            send(nxt, arr("LI", t + 1)[:, a:AU + 48], arr("OL", t)[:, a:AU + 48], "at%d" % (t + 1),
                 [("OB", t, 2), ("RU", t)] + [("OL", t, 3)] * MERGE)

    def Scat(t, q):
        if t < ST - 1:
            op("v", lambda: V.tensor_copy(T.Cx[:].indirect(arr("OL", t)[:, AU + 16:AU + 32]), T.NEW[:]),
               r=[("RU", t)] + [("NEW", k) for k in range(NQ)], w=call)

    parts = {"I": Ig, "i": Ih, "A": Gp, "L": Lg, "K": Lh, "l": Lv, "M": Mx(0), "N": Mx(1), "X": Ux(0), "Y": Ux(1), "U": Um(0), "V": Um(1), "E": Ur(0), "F": Ur(1), "W": Wm(0), "Z": Wm(1),
             "S": Sc, "k": Sk, "C": Cg, "c": Cv, "R": Rl, "P": PTI,
             "m": Cm, "G": Ge, "g": Gb, "B": Pb, "f": Fd, "Q": Pq, "J": Sj, "o": Po, "O": So, "u": Pu, "v": Vu, "w": Pw, "y": Vy, "z": Tail, "x": Scat}
    for t, order in [(0, ORDER)]:
        for tok in order.split():
            parts[tok[0]](*divmod(int(tok[1:]), NQ))

    for a, e in zip(OUTS, OUTS[1:]):
        wait("y", "ay%d" % a, len(topo.engines(prv, core)))
        g.sync.dma_start(T.yi[:, CH * a:CH * e], T.YL[:, CH * a:CH * e]).then_inc(T.sem.dout, 16)
    wait("s", "ay%d" % OUTS[-2], len(topo.engines(prv, core)))
    S.dma_start(T.yc[:], T.YL[:, NC:NC + 16]).then_inc(T.sem.dyc, 16)
    wait("s", "dyc", 16)
    wait("y", "dout", 16 * (len(OUTS) - 1))
    for q in own:
        wait("g", own[q], cnt[q])
    wait("g", "loc", tot["loc"])
